import numpy as np
import ml_dtypes


def mxq(x, axis, fmt="e4m3"):
    dtype, down = {"e4m3": (ml_dtypes.float8_e4m3fn, 7), "e5m2": (ml_dtypes.float8_e5m2, 14)}[fmt]
    v = np.moveaxis(np.asarray(x, np.float32).astype(ml_dtypes.bfloat16).astype(np.float64), axis, -1)
    blocks = v.reshape(v.shape[:-1] + (-1, 32))
    amax = np.abs(blocks).max(-1, keepdims=True)
    byte = np.maximum(np.where(amax > 0, np.frexp(amax)[1] - 1 + 127, 0) - down, 1)
    scale = np.exp2(byte - 127.0)
    codes = (blocks / scale).astype(np.float32).astype(dtype).astype(np.float64)
    return np.moveaxis((codes * scale).reshape(v.shape), -1, axis)


WIDE = False


def mx_kscale(k):
    if not WIDE:
        return np.ones(k)
    levels = np.array([10, -10, 5, -5, 0])
    if k % 512:
        return np.exp2(np.random.permutation(np.resize(levels, k // 32))).repeat(32)
    a = np.empty((k // 512, 16))
    for p in range(k // 512):
        a[p, :8] = np.random.permutation(np.resize(levels, 8))
        for g in range(8):
            far = levels[np.abs(levels - a[p, g]) >= 10]
            a[p, g + 8] = far[np.random.randint(len(far))]
    return np.exp2(a.ravel()).repeat(32)


BF16 = ml_dtypes.bfloat16


def bf(x):
    return np.asarray(x, np.float32).astype(BF16)


def f64(x):
    return np.asarray(x).astype(np.float64)


E2M1 = np.array([0.0, 0.5, 1.0, 1.5, 2.0, 3.0, 4.0, 6.0, -0.0, -0.5, -1.0, -1.5, -2.0, -3.0, -4.0, -6.0])


def pack_weight(w, fmt):
    k, n = w.shape
    w = f64(bf(w)).reshape(k // 32, 32, n)
    amax = np.abs(w).max(1)
    if fmt == "e4m3":
        byte = np.frexp(amax)[1] - 1 + 127 - 7
    else:
        mant, ex = np.frexp(amax / 6.0)
        byte = np.where(mant > 0.5, ex, ex - 1) + 127
    byte = np.clip(np.where(amax > 0, byte, 1), 1, 254)
    scaled = (w * np.exp2(127.0 - byte)[:, None, :]).reshape(k, n).astype(np.float32)
    by_word = np.ascontiguousarray(scaled.reshape(k // 512, 128, 4, n).transpose(0, 1, 3, 2))
    if fmt == "e4m3":
        words = by_word.astype(ml_dtypes.float8_e4m3fn).view(np.uint8)
    else:
        c = by_word.astype(ml_dtypes.float4_e2m1fn).view(np.uint8) & 0xF
        words = c[..., 0::2] | (c[..., 1::2] << 4)
    return np.ascontiguousarray(words), np.ascontiguousarray(byte.astype(np.uint8).reshape(k // 512, 16, n))


def unpack_weight(words, scales, fmt):
    g, p, n, _ = words.shape
    if fmt == "e4m3":
        vals = np.ascontiguousarray(words).view(ml_dtypes.float8_e4m3fn).astype(np.float64)
    else:
        nib = np.empty((g, p, n, 4), np.uint8)
        nib[..., 0::2] = words & 0xF
        nib[..., 1::2] = words >> 4
        vals = E2M1[nib]
    vals = vals * np.repeat(np.exp2(scales.astype(np.float64) - 127.0), 8, axis=1)[..., None]
    return vals.transpose(0, 1, 3, 2).reshape(g * 512, n)
def pack4(w):
    words, scales = pack_weight(w, "e2m1")
    return words.reshape(words.shape[0], 128, -1), scales


def unpack4(words, scales):
    return unpack_weight(words.reshape(words.shape[0], 128, -1, 2), scales, "e2m1")


B, O, V = 1536, 512, 1024


def draw0():
    s, t, u = mx_kscale(B), mx_kscale(B), mx_kscale(O)
    c_occ = bf(np.random.standard_normal((B, O)) / np.sqrt(B) * s[:, None])
    fock = bf(np.random.standard_normal((B, B)) / s[:, None] * t)
    occ = bf(np.random.uniform(0.5, 2.0, O) * u)
    c_virt_words, c_virt_scales = pack4(np.random.standard_normal((B, V)) / np.sqrt(B) / t[:, None])
    sc_occ = bf(np.random.standard_normal((B, O)) / np.sqrt(O) / u)
    e_occ = bf(-0.5 - np.random.uniform(0.0, 1.5, O))
    e_virt = bf(0.2 + np.random.uniform(0.0, 1.5, V))
    return {"c_occ": c_occ, "fock": fock, "occ": occ,
            "c_virt_words": c_virt_words, "c_virt_scales": c_virt_scales,
            "sc_occ": sc_occ, "e_occ": e_occ, "e_virt": e_virt}


def core(c_occ, fock, occ, c_virt_words, c_virt_scales, sc_occ, e_occ, e_virt):
    half = mxq(f64(c_occ), 0, "e4m3").T @ mxq(f64(fock), 0, "e4m3")
    h = half * f64(occ)[:, None]
    grad = mxq(h, 1, "e4m3") @ unpack4(c_virt_words, c_virt_scales)
    kappa = grad / (f64(e_occ)[:, None] - f64(e_virt)[None, :])
    spf = mxq(f64(sc_occ), 1, "e4m3") @ mxq(h, 0, "e4m3")
    return kappa, spf


def e4m3fn_bytes(y):
    return np.clip(np.asarray(y, np.float64), -448.0, 448.0).astype(np.float32).astype(ml_dtypes.float8_e4m3fn).view(np.uint8)


def e4m3fn_values(b):
    return np.asarray(b, np.uint8).view(ml_dtypes.float8_e4m3fn).astype(np.float64)


def setup_inputs():
    d = draw0()
    x0 = np.asarray(d['sc_occ']).astype(np.float64)
    s = (np.max(np.abs(x0), axis=(0,), keepdims=True) / 448.0).astype(np.float32)
    out = {}
    for k, v in d.items():
        if k == 'sc_occ':
            out['sc_occ_bytes'] = e4m3fn_bytes(x0 / s.astype(np.float64))
            out['sc_occ_scale'] = s
        else:
            out[k] = v
    return out


def reference(c_occ, fock, occ, c_virt_words, c_virt_scales, sc_occ_bytes, sc_occ_scale, e_occ, e_virt):
    return core(c_occ, fock, occ, c_virt_words, c_virt_scales, e4m3fn_values(sc_occ_bytes) * sc_occ_scale.astype(np.float64), e_occ, e_virt)

@@ -1,0 +1,589 @@
+from contextlib import ExitStack
+
+import concourse.mybir as mybir
+from concourse.masks import make_identity
+
+F32 = mybir.dt.float32
+BF16 = mybir.dt.bfloat16
+I32 = mybir.dt.int32
+U32 = mybir.dt.uint32
+U8 = mybir.dt.uint8
+FP8 = mybir.dt.float8_e4m3fn
+FP8X4 = mybir.dt.float8_e4m3fn_x4
+FP4X4 = mybir.dt.float4_e2m1fn_x4
+ACT = mybir.ActivationFunctionType
+ALU = mybir.AluOpType
+
+P = 128
+PACK = 4
+B, O, V = 1536, 512, 1024
+G = B // 512
+NB = 512
+RT = B // P
+FLOPS = 2 * O * B * B + 2 * O * B * V + 2 * B * O * B
+
+
+def tile_orbital_rotation_gradient_s8_kernel(
+    tc, c_occ, fock, occ, c_virt_words, c_virt_scales, sc_bytes, sc_scale, e_occ, e_virt, kappa, spf
+):
+    nc = tc.nc
+    with ExitStack() as ctx:
+        keep = ctx.enter_context(tc.tile_pool(name="keep", bufs=1))
+        work = ctx.enter_context(tc.tile_pool(name="work", bufs=3))
+        outs = ctx.enter_context(tc.tile_pool(name="outs", bufs=6))
+        mm = ctx.enter_context(tc.psum_pool(name="mm", bufs=6))
+        tr = ctx.enter_context(tc.psum_pool(name="tr", bufs=2))
+
+        scale_row = keep.tile([P, O], F32, name="scale_row")
+        virt_row = keep.tile([P, V], BF16, name="virt_row")
+        ones_f = keep.tile([P, P], F32, name="ones_f")
+        ones_b = keep.tile([P, P], BF16, name="ones_b")
+        ident = keep.tile([P, P], F32, name="ident")
+        occ_b = keep.tile([P, PACK], BF16, name="occ_b")
+        eocc_b = keep.tile([P, PACK], BF16, name="eocc_b")
+        occ_f = keep.tile([P, PACK], F32, name="occ_f")
+        eocc_f = keep.tile([P, PACK], F32, name="eocc_f")
+        scale_all = keep.tile([P, O], F32, name="scale_all")
+        virt_all = keep.tile([P, V], BF16, name="virt_all")
+        below = keep.tile([P, PACK, V], BF16, name="below")
+        ident_b = keep.tile([P, P], BF16, name="ident_b")
+        rgap = keep.tile([P, PACK, V], F32, name="rgap")
+        warm = keep.tile([P, 1], F32, name="warm")
+        c_raw = [keep.tile([P, PACK, O], BF16, name=f"c_raw{g}") for g in range(G)]
+        f_raw0 = [keep.tile([P, PACK, NB], BF16, name=f"f_raw0_{g}") for g in range(G)]
+        f_raw1 = [keep.tile([P, PACK, 2 * NB], BF16, name=f"f_raw1_{g}") for g in range(G)]
+        sc_raw = [keep.tile([P, RT // 2, O], U8, name=f"sc_raw{h}") for h in range(2)]
+        cv_words = keep.tile([P, G, 2 * V], U8, name="cv_words", align_bytes=64)
+        cv_scales = keep.tile([P, G, V], U8, name="cv_scales", align_bytes=64)
+        c_codes = keep.tile([P, G, O], U32, name="c_codes", align_bytes=64)
+        c_scales = keep.tile([P, G, O], U8, name="c_scales", align_bytes=64)
+        f_codes = keep.tile([P, G, B], U32, name="f_codes", align_bytes=64)
+        f_scales = keep.tile([P, G, B], U8, name="f_scales", align_bytes=64)
+        h_bf = keep.tile([P, PACK, B], BF16, name="h_bf", align_bytes=64)
+        h_codes = keep.tile([P, B], U32, name="h_codes", align_bytes=64)
+        h_scales = keep.tile([P, B], U8, name="h_scales", align_bytes=64)
+        ht_codes = keep.tile([P, G, O], U32, name="ht_codes", align_bytes=64)
+        ht_scales = keep.tile([P, G, O], U8, name="ht_scales", align_bytes=64)
+        s_codes = keep.tile([P, B], U32, name="s_codes", align_bytes=64)
+        s_scales = keep.tile([P, B], U8, name="s_scales", align_bytes=64)
+
+        c_view = c_occ.rearrange("(g p j) o -> g p j o", p=P, j=PACK)
+        f_view = fock.rearrange("(g p j) n -> g p j n", p=P, j=PACK)
+        sc_view = sc_bytes.rearrange("(p i) o -> p i o", i=RT)
+        spf_view = spf.rearrange("(p i) n -> p i n", i=RT)
+        kappa_view = kappa.rearrange("(p t) v -> p t v", t=PACK)
+
+        def copy(engine, out, in_):
+            if engine == "v":
+                nc.vector.tensor_copy(out=out, in_=in_)
+            else:
+                nc.scalar.copy(out=out, in_=in_)
+
+        grouped = {}
+
+        def new_grouped(key):
+            t = work.tile([P, NB, PACK], BF16, name="grouped", align_bytes=64, bufs=5)
+            grouped[key] = t
+            return t
+
+        def flat(key):
+            return grouped[key][:].rearrange("p c t -> p (c t)")
+
+        spread_ps = {}
+
+        def raw_view(key):
+            if key[0] == "c":
+                return c_raw[key[1]][:].rearrange("p j (m t) -> p t m j", t=PACK)
+            g, n = key[1:]
+            src = f_raw0[g][:] if n == 0 else f_raw1[g][:, :, (n - 1) * NB : n * NB]
+            return src.rearrange("p j (t m) -> p t m j", t=PACK)
+
+        def spread(key, half):
+            ps = mm.tile([P, 2 * NB], BF16, name="ps")
+            spread_ps[key, half] = ps
+            for k in range(2):
+                nc.tensor.matmul(
+                    out=ps[:, k * NB : (k + 1) * NB].rearrange("p (c t) -> p c t", t=PACK),
+                    lhsT=ident_b[:],
+                    rhs=raw_view(key)[:, 2 * half + k, :, :],
+                    start=True,
+                    stop=True,
+                )
+
+        def spread_out(key, half, engine):
+            if key not in grouped:
+                new_grouped(key)
+            copy(
+                engine,
+                grouped[key][:, half * 256 : (half + 1) * 256, :].rearrange("p c t -> p (c t)"),
+                spread_ps[key, half][:],
+            )
+
+        def group_c(g, engine):
+            dst = new_grouped(("c", g))
+            copy(
+                engine,
+                dst[:].rearrange("p (t m) j -> p t m j", t=PACK),
+                c_raw[g][:].rearrange("p j (m t) -> p t m j", t=PACK),
+            )
+
+        def quant_c(g):
+            nc.vector.quantize_mx(
+                out=c_codes[:, g, :].bitcast(FP8X4), scales=c_scales[:, g, :], in_=flat(("c", g))
+            )
+
+        def group_f(g, n, engine):
+            dst = new_grouped(("f", g, n))
+            src = f_raw0[g][:] if n == 0 else f_raw1[g][:, :, (n - 1) * NB : n * NB]
+            copy(
+                engine,
+                dst[:].rearrange("p (c i) t -> p c t i", i=4),
+                src.rearrange("p t (c i) -> p c t i", i=4),
+            )
+
+        def quant_f(g, n):
+            cols = slice(n * NB, (n + 1) * NB)
+            nc.vector.quantize_mx(
+                out=f_codes[:, g, cols].bitcast(FP8X4), scales=f_scales[:, g, cols], in_=flat(("f", g, n))
+            )
+
+        half = {}
+
+        def half_mm(n, tiles, groups):
+            cols = slice(n * NB, (n + 1) * NB)
+            for t in tiles:
+                for g in groups:
+                    if g == 0:
+                        ps = mm.tile([P, NB], F32, name="ps")
+                        half[n, t] = ps
+                    nc.tensor.matmul_mx(
+                        out=half[n, t][:],
+                        lhsT=c_codes[:, g, t * P : (t + 1) * P].bitcast(FP8X4),
+                        lhsT_scale=c_scales[:, g, t * P : (t + 1) * P],
+                        rhs=f_codes[:, g, cols].bitcast(FP8X4),
+                        rhs_scale=f_scales[:, g, cols],
+                        start=(g == 0),
+                        stop=(g == G - 1),
+                    )
+
+        def h_out(n, t, engine):
+            cols = slice(n * NB, (n + 1) * NB)
+            if engine == "v":
+                nc.vector.tensor_scalar(
+                    out=h_bf[:, t, cols], in0=half[n, t][:], scalar1=occ_f[:, t : t + 1], scalar2=None, op0=ALU.mult
+                )
+            else:
+                nc.scalar.activation(
+                    out=h_bf[:, t, cols], in_=half[n, t][:], func=ACT.Copy, scale=occ_f[:, t : t + 1]
+                )
+
+        def group_h(n, engine):
+            dst = new_grouped(("h", n))
+            copy(
+                engine,
+                dst[:].rearrange("p (c i) t -> p c t i", i=4),
+                h_bf[:, :, n * NB : (n + 1) * NB].rearrange("p t (c i) -> p c t i", i=4),
+            )
+
+        def quant_h(n):
+            cols = slice(n * NB, (n + 1) * NB)
+            nc.vector.quantize_mx(
+                out=h_codes[:, cols].bitcast(FP8X4), scales=h_scales[:, cols], in_=flat(("h", n))
+            )
+
+        turned = {}
+
+        def turn_h(n, pair):
+            ps = tr.tile([P, 4, P], F32, name="pt")
+            turned["h", n, pair] = ps
+            for k in range(2):
+                words = h_bf[:, 2 * pair + k, n * NB : (n + 1) * NB].bitcast(F32)
+                for u in range(2):
+                    nc.tensor.transpose(ps[:, 2 * k + u, :], words[:, u : NB // 2 : 2], ident[:])
+
+        def turned_out(what, n, pair, engine):
+            key = (what + "t", n)
+            if key not in grouped:
+                t = work.tile([P, NB, PACK], BF16, name=what + "_turned", align_bytes=64, bufs=2)
+                grouped[key] = t
+            words = grouped[key][:].rearrange("p c t -> p (c t)").bitcast(F32)
+            copy(
+                engine,
+                words[:, pair * NB : (pair + 1) * NB].rearrange("p (k r u) -> p k r u", k=2, u=2),
+                turned[what, n, pair][:].rearrange("p (k u) r -> p k r u", k=2),
+            )
+
+        def quant_ht(n):
+            nc.vector.quantize_mx(
+                out=ht_codes[:, n, :].bitcast(FP8X4), scales=ht_scales[:, n, :], in_=flat(("ht", n))
+            )
+
+        sc_bf = {}
+
+        def product(i):
+            if i // 4 not in sc_bf:
+                t = work.tile([P, 4, O], BF16, name="sc_bf", bufs=3)
+                sc_bf[i // 4] = t
+            nc.vector.tensor_tensor(
+                out=sc_bf[i // 4][:, i % 4, :],
+                in0=sc_raw[i // (RT // 2)][:, i % (RT // 2), :].bitcast(FP8),
+                in1=scale_all[:],
+                op=ALU.mult,
+            )
+
+        def turn_s(c, pair):
+            ps = tr.tile([P, 4, P], F32, name="pt")
+            turned["s", c, pair] = ps
+            for k in range(2):
+                words = sc_bf[c][:, 2 * pair + k, :].bitcast(F32)
+                for u in range(2):
+                    nc.tensor.transpose(ps[:, 2 * k + u, :], words[:, u : O // 2 : 2], ident[:])
+
+        def quant_s(c):
+            cols = slice(c * NB, (c + 1) * NB)
+            nc.vector.quantize_mx(
+                out=s_codes[:, cols].bitcast(FP8X4), scales=s_scales[:, cols], in_=flat(("st", c))
+            )
+
+        prod = {}
+
+        def spf_mm(n, i):
+            ps = mm.tile([P, NB], F32, name="ps")
+            prod[n, i] = ps
+            cols = slice(n * NB, (n + 1) * NB)
+            nc.tensor.matmul_mx(
+                out=ps[:],
+                lhsT=s_codes[:, i * P : (i + 1) * P].bitcast(FP8X4),
+                lhsT_scale=s_scales[:, i * P : (i + 1) * P],
+                rhs=h_codes[:, cols].bitcast(FP8X4),
+                rhs_scale=h_scales[:, cols],
+                start=True,
+                stop=True,
+            )
+
+        staged = {}
+
+        def spf_out(n, i, engine):
+            first = (n, i // 2) not in staged
+            if first:
+                t = outs.tile([P, 2, NB], F32, name="staged")
+                staged[n, i // 2] = t
+            copy(engine, staged[n, i // 2][:, i % 2, :], prod[n, i][:])
+            if not first:
+                spf_store(n, i // 2)
+
+        def spf_store(n, j):
+            nc.sync.dma_start(
+                out=spf_view[:, 2 * j : 2 * j + 2, n * NB : (n + 1) * NB], in_=staged[n, j][:]
+            )
+
+        grad = {}
+
+        def kappa_mm(t, v):
+            ps = mm.tile([P, NB], F32, name="ps")
+            grad[t, v] = ps
+            for g in range(G):
+                nc.tensor.matmul_mx(
+                    out=ps[:],
+                    lhsT=ht_codes[:, g, t * P : (t + 1) * P].bitcast(FP8X4),
+                    lhsT_scale=ht_scales[:, g, t * P : (t + 1) * P],
+                    rhs=cv_words[:, g, 2 * NB * v : 2 * NB * (v + 1)].bitcast(FP4X4),
+                    rhs_scale=cv_scales[:, g, NB * v : NB * (v + 1)],
+                    start=(g == 0),
+                    stop=(g == G - 1),
+                )
+
+        kappa_done = {}
+
+        def kappa_out(t, v):
+            cols = slice(v * NB, (v + 1) * NB)
+            nc.vector.tensor_tensor(out=rgap[:, t, cols], in0=grad[t, v][:], in1=rgap[:, t, cols], op=ALU.mult)
+            if t in kappa_done:
+                kappa_store(t)
+            kappa_done[t] = v
+
+        def kappa_store(t):
+            nc.sync.dma_start(out=kappa_view[:, t, :], in_=rgap[:, t, :])
+
+
+        def bcast(ones, row, dst):
+            ps = mm.tile([P, NB], F32, name="ps")
+            nc.tensor.matmul(out=ps[:], lhsT=ones[:], rhs=row, start=True, stop=True)
+            nc.scalar.copy(out=dst, in_=ps[:])
+
+        def recip(t):
+            nc.vector.scalar_tensor_tensor(
+                out=rgap[:, t, :], in0=below[:, t, :], scalar=1.0, in1=rgap[:, t, :], op0=ALU.subtract, op1=ALU.mult
+            )
+
+        def root(t):
+            nc.scalar.activation(
+                out=rgap[:, t, :], in_=virt_all[:], func=ACT.Abs_reciprocal_sqrt, scale=-1.0, bias=eocc_f[:, t : t + 1]
+            )
+
+        def square(t):
+            nc.scalar.activation(out=rgap[:, t, :], in_=rgap[:, t, :], func=ACT.Square)
+
+        def spf_tile(n, i, engine):
+            spf_mm(n, i)
+            spf_out(n, i, engine)
+
+        def product_run(*rows):
+            for i in rows:
+                product(i)
+
+        with tc.manual_schedule():
+            nc.vector.memset(scale_row[:], 0.0)
+            nc.vector.memset(ones_f[:], 1.0)
+            nc.vector.memset(virt_row[:], 0.0)
+            nc.vector.memset(ones_b[:], 1.0)
+            nc.vector.memset(warm[:], 1.0)
+            nc.vector.memset(cv_scales[:].rearrange("p g v -> p (g v)").bitcast(I32), 0)
+            make_identity(nc, ident[:])
+            make_identity(nc, ident_b[:])
+            nc.scalar.dma_start(out=scale_row[0:1, :], in_=sc_scale)
+            nc.scalar.dma_start(out=eocc_b[:], in_=e_occ.rearrange("(p t) -> p t", t=PACK))
+            nc.scalar.dma_start(out=occ_b[:], in_=occ.rearrange("(p t) -> p t", t=PACK))
+            nc.scalar.dma_start(out=virt_row[0:1, :], in_=e_virt.rearrange("(o v) -> o v", o=1))
+            nc.scalar.activation(out=warm[:], in_=warm[:], func=ACT.Abs_reciprocal_sqrt)
+            for g in range(G):
+                nc.sync.dma_start(out=c_raw[g][:], in_=c_view[g])
+            nc.sync.dma_start(out=sc_raw[0][:], in_=sc_view[:, : RT // 2, :])
+            for g in range(G):
+                nc.sync.dma_start(out=f_raw0[g][:], in_=f_view[g, :, :, :NB])
+            nc.sync.dma_start(out=sc_raw[1][:], in_=sc_view[:, RT // 2 :, :])
+            for g in range(G):
+                nc.sync.dma_start(out=f_raw1[g][:], in_=f_view[g, :, :, NB:])
+            nc.sync.dma_start(out=cv_words[:], in_=c_virt_words.rearrange("g p n -> p g n"))
+            for q in range(4):
+                nc.sync.dma_start(
+                    out=cv_scales[32 * q : 32 * q + 4, :, :].bitcast(I32),
+                    in_=c_virt_scales[:, 4 * q : 4 * q + 4, :].bitcast(I32).rearrange("g q v -> q g v"),
+                )
+            bcast(ones_f, scale_row[:], scale_all[:])
+            bcast(ones_b, virt_row[:, :NB], virt_all[:, :NB])
+            bcast(ones_b, virt_row[:, NB:], virt_all[:, NB:])
+            nc.vector.tensor_copy(out=eocc_f[:], in_=eocc_b[:])
+            nc.vector.tensor_copy(out=occ_f[:], in_=occ_b[:])
+            for t in range(PACK):
+                nc.gpsimd.tensor_scalar(
+                    out=below[:, t, :], in0=virt_all[:], scalar1=eocc_f[:, t : t + 1], scalar2=2.0,
+                    op0=ALU.is_lt, op1=ALU.mult,
+                )
+            group_c(0, "v")
+            spread(("c", 1), 1)
+            quant_c(0)
+            spread(("c", 1), 0)
+            root(1)
+            spread_out(("c", 1), 1, "v")
+            spread(("c", 2), 1)
+            spread_out(("c", 1), 0, "v")
+            spread(("c", 2), 0)
+            root(0)
+            spread_out(("c", 2), 1, "v")
+            quant_c(1)
+            spread_out(("c", 2), 0, "s")
+            product(3)
+            spread(("f", 0, 0), 1)
+            square(0)
+            product(2)
+            spread(("f", 0, 0), 0)
+            spread_out(("f", 0, 0), 1, "v")
+            turn_s(0, 1)
+            square(1)
+            quant_c(2)
+            group_f(1, 0, "v")
+            turned_out("s", 0, 1, "s")
+            spread(("f", 2, 0), 1)
+            product(0)
+            spread_out(("f", 0, 0), 0, "s")
+            quant_f(1, 0)
+            root(2)
+            spread(("f", 2, 0), 0)
+            spread_out(("f", 2, 0), 1, "v")
+            spread_out(("f", 2, 0), 0, "v")
+            root(3)
+            quant_f(0, 0)
+            quant_f(2, 0)
+            square(2)
+            spread(("f", 0, 2), 1)
+            product(1)
+            half_mm(0, [1], range(G))
+            group_f(0, 1, "s")
+            product(4)
+            product(6)
+            half_mm(0, [0], range(G))
+            h_out(0, 1, "v")
+            half_mm(0, [3], range(G))
+            product(5)
+            h_out(0, 0, "s")
+            product(7)
+            half_mm(0, [2], range(G))
+            h_out(0, 3, "s")
+            product(11)
+            turn_s(0, 0)
+            group_f(1, 2, "s")
+            product(9)
+            turn_s(1, 1)
+            h_out(0, 2, "v")
+            spread(("f", 1, 1), 0)
+            turned_out("s", 0, 0, "v")
+            group_h(0, "v")
+            spread(("f", 2, 1), 0)
+            turned_out("s", 1, 1, "s")
+            turn_s(1, 0)
+            spread_out(("f", 2, 1), 0, "s")
+            quant_s(0)
+            spread(("f", 2, 1), 1)
+            spread_out(("f", 1, 1), 0, "s")
+            quant_h(0)
+            spread(("f", 1, 1), 1)
+            turned_out("s", 1, 0, "s")
+            product(10)
+            spf_mm(0, 0)
+            spread_out(("f", 2, 1), 1, "s")
+            product(8)
+            spf_mm(0, 1)
+            spf_mm(0, 2)
+            spf_out(0, 0, "s")
+            spread_out(("f", 1, 1), 1, "v")
+            spf_mm(0, 3)
+            spf_out(0, 1, "s")
+            turn_s(2, 0)
+            quant_s(1)
+            spf_out(0, 2, "s")
+            turn_s(2, 1)
+            spf_out(0, 3, "v")
+            turned_out("s", 2, 0, "s")
+            spf_mm(0, 4)
+            quant_f(0, 1)
+            spf_mm(0, 5)
+            turned_out("s", 2, 1, "s")
+            quant_f(2, 1)
+            spf_mm(0, 6)
+            spf_mm(0, 7)
+            spf_out(0, 4, "s")
+            quant_f(1, 1)
+            spread(("f", 0, 2), 0)
+            spf_out(0, 5, "s")
+            quant_s(2)
+            turn_h(0, 0)
+            spf_out(0, 7, "s")
+            group_f(2, 2, "v")
+            half_mm(1, [1], range(G))
+            spread_out(("f", 0, 2), 1, "s")
+            spread_out(("f", 0, 2), 0, "s")
+            spf_out(0, 6, "v")
+            half_mm(1, [2], range(G))
+            h_out(1, 1, "s")
+            quant_f(1, 2)
+            half_mm(1, [3], range(G))
+            turned_out("h", 0, 0, "s")
+            quant_f(0, 2)
+            h_out(1, 2, "s")
+            quant_f(2, 2)
+            half_mm(1, [0], range(G))
+            h_out(1, 3, "s")
+            recip(0)
+            spf_mm(0, 8)
+            square(3)
+            spf_mm(0, 9)
+            spf_mm(0, 10)
+            h_out(1, 0, "v")
+            spf_mm(0, 11)
+            half_mm(2, [2], range(G))
+            spf_out(0, 8, "s")
+            spf_out(0, 9, "v")
+            spf_out(0, 11, "s")
+            group_h(1, "v")
+            half_mm(2, [0], range(G))
+            spf_out(0, 10, "s")
+            h_out(2, 2, "v")
+            half_mm(2, [1], range(G))
+            h_out(2, 0, "s")
+            quant_h(1)
+            half_mm(2, [3], range(G))
+            h_out(2, 1, "s")
+            recip(1)
+            spf_mm(1, 0)
+            h_out(2, 3, "s")
+            spf_mm(1, 1)
+            spf_mm(1, 2)
+            spf_out(1, 0, "v")
+            spf_out(1, 1, "s")
+            spf_mm(1, 3)
+            spf_mm(1, 4)
+            group_h(2, "v")
+            spf_out(1, 2, "s")
+            spf_mm(1, 5)
+            spf_mm(1, 6)
+            spf_out(1, 3, "s")
+            spf_mm(1, 7)
+            spf_out(1, 4, "v")
+            spf_mm(1, 8)
+            spf_out(1, 5, "s")
+            turn_h(0, 1)
+            spf_out(1, 6, "v")
+            spf_out(1, 7, "s")
+            quant_h(2)
+            spf_mm(1, 9)
+            spf_out(1, 8, "s")
+            spf_mm(1, 10)
+            turned_out("h", 0, 1, "v")
+            spf_mm(1, 11)
+            spf_out(1, 10, "s")
+            spf_mm(2, 0)
+            spf_out(1, 9, "v")
+            spf_mm(2, 1)
+            spf_out(1, 11, "s")
+            spf_mm(2, 2)
+            spf_out(2, 0, "v")
+            turn_h(1, 0)
+            spf_out(2, 1, "s")
+            spf_out(2, 2, "v")
+            turn_h(1, 1)
+            turned_out("h", 1, 0, "s")
+            quant_ht(0)
+            spf_mm(2, 3)
+            turned_out("h", 1, 1, "s")
+            recip(2)
+            spf_mm(2, 4)
+            turn_h(2, 1)
+            spf_out(2, 3, "s")
+            turn_h(2, 0)
+            spf_out(2, 4, "s")
+            quant_ht(1)
+            spf_mm(2, 5)
+            turned_out("h", 2, 1, "s")
+            recip(3)
+            spf_mm(2, 6)
+            turned_out("h", 2, 0, "s")
+            spf_mm(2, 7)
+            spf_mm(2, 8)
+            spf_out(2, 5, "s")
+            spf_out(2, 6, "v")
+            spf_mm(2, 9)
+            spf_mm(2, 10)
+            spf_out(2, 7, "s")
+            quant_ht(2)
+            spf_mm(2, 11)
+            spf_out(2, 8, "s")
+            spf_out(2, 9, "v")
+            kappa_mm(0, 0)
+            spf_out(2, 10, "s")
+            spf_out(2, 11, "v")
+            kappa_mm(0, 1)
+            kappa_out(0, 0)
+            kappa_mm(1, 0)
+            kappa_out(0, 1)
+            kappa_mm(1, 1)
+            kappa_out(1, 0)
+            kappa_mm(2, 0)
+            kappa_out(1, 1)
+            kappa_mm(2, 1)
+            kappa_out(2, 0)
+            kappa_mm(3, 0)
+            kappa_out(2, 1)
+            kappa_mm(3, 1)
+            kappa_out(3, 0)
+            kappa_out(3, 1)

@@ -30,7 +30,7 @@ def tile_orbital_rotation_gradient_s8_kernel(
     with ExitStack() as ctx:
         keep = ctx.enter_context(tc.tile_pool(name="keep", bufs=1))
         work = ctx.enter_context(tc.tile_pool(name="work", bufs=3))
-        outs = ctx.enter_context(tc.tile_pool(name="outs", bufs=6))
+        outs = ctx.enter_context(tc.tile_pool(name="outs", bufs=12))
         mm = ctx.enter_context(tc.psum_pool(name="mm", bufs=6))
         tr = ctx.enter_context(tc.psum_pool(name="tr", bufs=2))
 
@@ -49,8 +49,8 @@ def tile_orbital_rotation_gradient_s8_kernel(
         ident_b = keep.tile([P, P], BF16, name="ident_b")
         rgap = keep.tile([P, PACK, V], F32, name="rgap")
         warm = keep.tile([P, 1], F32, name="warm")
-        c_raw = [keep.tile([P, PACK, O], BF16, name=f"c_raw{g}") for g in range(G)]
-        f_raw0 = [keep.tile([P, PACK, NB], BF16, name=f"f_raw0_{g}") for g in range(G)]
+        c_raw = [outs.tile([P, PACK, O], BF16, name="staged") for g in range(G)]
+        f_raw0 = [outs.tile([P, PACK, NB], BF16, name="staged") for g in range(G)]
         f_raw1 = [keep.tile([P, PACK, 2 * NB], BF16, name=f"f_raw1_{g}") for g in range(G)]
         sc_raw = [keep.tile([P, RT // 2, O], U8, name=f"sc_raw{h}") for h in range(2)]
         cv_words = keep.tile([P, G, 2 * V], U8, name="cv_words", align_bytes=64)
@@ -204,7 +204,7 @@ def tile_orbital_rotation_gradient_s8_kernel(
         def turned_out(what, n, pair, engine):
             key = (what + "t", n)
             if key not in grouped:
-                t = work.tile([P, NB, PACK], BF16, name=what + "_turned", align_bytes=64, bufs=2)
+                t = work.tile([P, NB, PACK], BF16, name="turned_sb", align_bytes=64, bufs=4)
                 grouped[key] = t
             words = grouped[key][:].rearrange("p c t -> p (c t)").bitcast(F32)
             copy(
@@ -316,9 +316,14 @@ def tile_orbital_rotation_gradient_s8_kernel(
                 out=rgap[:, t, :], in0=below[:, t, :], scalar=1.0, in1=rgap[:, t, :], op0=ALU.subtract, op1=ALU.mult
             )
 
+        def side(t):
+            nc.vector.tensor_scalar(
+                out=below[:, t, :], in0=virt_all[:], scalar1=eocc_b[:, t : t + 1], scalar2=2.0, op0=ALU.is_lt, op1=ALU.mult
+            )
+
         def root(t):
             nc.scalar.activation(
-                out=rgap[:, t, :], in_=virt_all[:], func=ACT.Abs_reciprocal_sqrt, scale=-1.0, bias=eocc_f[:, t : t + 1]
+                out=rgap[:, t, :], in_=virt_all[:], func=ACT.Abs_reciprocal_sqrt, scale=-1.0, bias=eocc_b[:, t : t + 1]
             )
 
         def square(t):
@@ -340,14 +345,14 @@ def tile_orbital_rotation_gradient_s8_kernel(
             nc.vector.memset(warm[:], 1.0)
             nc.vector.memset(cv_scales[:].rearrange("p g v -> p (g v)").bitcast(I32), 0)
             make_identity(nc, ident[:])
-            make_identity(nc, ident_b[:])
-            nc.scalar.dma_start(out=scale_row[0:1, :], in_=sc_scale)
-            nc.scalar.dma_start(out=eocc_b[:], in_=e_occ.rearrange("(p t) -> p t", t=PACK))
-            nc.scalar.dma_start(out=occ_b[:], in_=occ.rearrange("(p t) -> p t", t=PACK))
-            nc.scalar.dma_start(out=virt_row[0:1, :], in_=e_virt.rearrange("(o v) -> o v", o=1))
             nc.scalar.activation(out=warm[:], in_=warm[:], func=ACT.Abs_reciprocal_sqrt)
-            for g in range(G):
-                nc.sync.dma_start(out=c_raw[g][:], in_=c_view[g])
+            nc.sync.dma_start(out=c_raw[0][:], in_=c_view[0])
+            nc.sync.dma_start(out=scale_row[0:1, :], in_=sc_scale)
+            nc.sync.dma_start(out=virt_row[0:1, :], in_=e_virt.rearrange("(o v) -> o v", o=1))
+            nc.sync.dma_start(out=eocc_b[:], in_=e_occ.rearrange("(p t) -> p t", t=PACK))
+            nc.sync.dma_start(out=occ_b[:], in_=occ.rearrange("(p t) -> p t", t=PACK))
+            nc.sync.dma_start(out=c_raw[1][:], in_=c_view[1])
+            nc.sync.dma_start(out=c_raw[2][:], in_=c_view[2])
             nc.sync.dma_start(out=sc_raw[0][:], in_=sc_view[:, : RT // 2, :])
             for g in range(G):
                 nc.sync.dma_start(out=f_raw0[g][:], in_=f_view[g, :, :, :NB])
@@ -360,230 +365,207 @@ def tile_orbital_rotation_gradient_s8_kernel(
                     out=cv_scales[32 * q : 32 * q + 4, :, :].bitcast(I32),
                     in_=c_virt_scales[:, 4 * q : 4 * q + 4, :].bitcast(I32).rearrange("g q v -> q g v"),
                 )
-            bcast(ones_f, scale_row[:], scale_all[:])
-            bcast(ones_b, virt_row[:, :NB], virt_all[:, :NB])
-            bcast(ones_b, virt_row[:, NB:], virt_all[:, NB:])
-            nc.vector.tensor_copy(out=eocc_f[:], in_=eocc_b[:])
-            nc.vector.tensor_copy(out=occ_f[:], in_=occ_b[:])
-            for t in range(PACK):
-                nc.gpsimd.tensor_scalar(
-                    out=below[:, t, :], in0=virt_all[:], scalar1=eocc_f[:, t : t + 1], scalar2=2.0,
-                    op0=ALU.is_lt, op1=ALU.mult,
-                )
+            group_c(1, "s")
             group_c(0, "v")
-            spread(("c", 1), 1)
             quant_c(0)
-            spread(("c", 1), 0)
-            root(1)
-            spread_out(("c", 1), 1, "v")
-            spread(("c", 2), 1)
-            spread_out(("c", 1), 0, "v")
-            spread(("c", 2), 0)
-            root(0)
-            spread_out(("c", 2), 1, "v")
-            quant_c(1)
-            spread_out(("c", 2), 0, "s")
-            product(3)
-            spread(("f", 0, 0), 1)
-            square(0)
-            product(2)
-            spread(("f", 0, 0), 0)
-            spread_out(("f", 0, 0), 1, "v")
-            turn_s(0, 1)
-            square(1)
+            group_c(2, "v")
             quant_c(2)
-            group_f(1, 0, "v")
-            turned_out("s", 0, 1, "s")
-            spread(("f", 2, 0), 1)
+            quant_c(1)
+            nc.vector.tensor_copy(out=occ_f[:], in_=occ_b[:])
+            bcast(ones_f, scale_row[:], scale_all[:])
+            bcast(ones_b, virt_row[:, NB:], virt_all[:, NB:])
             product(0)
-            spread_out(("f", 0, 0), 0, "s")
+            product(1)
+            bcast(ones_b, virt_row[:, :NB], virt_all[:, :NB])
+            group_f(1, 0, "v")
+            product(2)
+            product(3)
+            product(6)
+            group_f(0, 0, "s")
+            group_f(2, 0, "s")
+            product(4)
+            turn_s(0, 0)
+            turn_s(0, 1)
+            turned_out("s", 0, 1, "s")
             quant_f(1, 0)
-            root(2)
-            spread(("f", 2, 0), 0)
-            spread_out(("f", 2, 0), 1, "v")
-            spread_out(("f", 2, 0), 0, "v")
-            root(3)
+            turned_out("s", 0, 0, "s")
             quant_f(0, 0)
             quant_f(2, 0)
-            square(2)
-            spread(("f", 0, 2), 1)
-            product(1)
-            half_mm(0, [1], range(G))
-            group_f(0, 1, "s")
-            product(4)
-            product(6)
-            half_mm(0, [0], range(G))
-            h_out(0, 1, "v")
+            group_f(0, 2, "v")
             half_mm(0, [3], range(G))
-            product(5)
-            h_out(0, 0, "s")
+            group_f(0, 1, "s")
+            half_mm(0, [1], range(G))
             product(7)
             half_mm(0, [2], range(G))
-            h_out(0, 3, "s")
-            product(11)
-            turn_s(0, 0)
-            group_f(1, 2, "s")
-            product(9)
-            turn_s(1, 1)
-            h_out(0, 2, "v")
-            spread(("f", 1, 1), 0)
-            turned_out("s", 0, 0, "v")
-            group_h(0, "v")
-            spread(("f", 2, 1), 0)
-            turned_out("s", 1, 1, "s")
+            product(5)
             turn_s(1, 0)
-            spread_out(("f", 2, 1), 0, "s")
-            quant_s(0)
-            spread(("f", 2, 1), 1)
-            spread_out(("f", 1, 1), 0, "s")
-            quant_h(0)
-            spread(("f", 1, 1), 1)
-            turned_out("s", 1, 0, "s")
-            product(10)
-            spf_mm(0, 0)
-            spread_out(("f", 2, 1), 1, "s")
-            product(8)
-            spf_mm(0, 1)
-            spf_mm(0, 2)
-            spf_out(0, 0, "s")
-            spread_out(("f", 1, 1), 1, "v")
-            spf_mm(0, 3)
-            spf_out(0, 1, "s")
-            turn_s(2, 0)
-            quant_s(1)
-            spf_out(0, 2, "s")
-            turn_s(2, 1)
-            spf_out(0, 3, "v")
-            turned_out("s", 2, 0, "s")
-            spf_mm(0, 4)
+            group_f(1, 1, "s")
             quant_f(0, 1)
-            spf_mm(0, 5)
-            turned_out("s", 2, 1, "s")
-            quant_f(2, 1)
-            spf_mm(0, 6)
-            spf_mm(0, 7)
-            spf_out(0, 4, "s")
+            group_f(1, 2, "s")
+            h_out(0, 3, "v")
+            turn_s(1, 1)
+            half_mm(0, [0], range(G))
+            h_out(0, 0, "s")
+            h_out(0, 2, "s")
+            h_out(0, 1, "s")
+            turned_out("s", 1, 1, "s")
+            group_f(2, 1, "v")
             quant_f(1, 1)
-            spread(("f", 0, 2), 0)
-            spf_out(0, 5, "s")
-            quant_s(2)
-            turn_h(0, 0)
-            spf_out(0, 7, "s")
-            group_f(2, 2, "v")
-            half_mm(1, [1], range(G))
-            spread_out(("f", 0, 2), 1, "s")
-            spread_out(("f", 0, 2), 0, "s")
-            spf_out(0, 6, "v")
-            half_mm(1, [2], range(G))
-            h_out(1, 1, "s")
-            quant_f(1, 2)
-            half_mm(1, [3], range(G))
-            turned_out("h", 0, 0, "s")
-            quant_f(0, 2)
-            h_out(1, 2, "s")
-            quant_f(2, 2)
+            quant_f(2, 1)
+            turned_out("s", 1, 0, "s")
             half_mm(1, [0], range(G))
+            half_mm(1, [2], range(G))
+            half_mm(1, [3], range(G))
+            half_mm(1, [1], range(G))
+            group_f(2, 2, "v")
+            quant_f(0, 2)
             h_out(1, 3, "s")
-            recip(0)
-            spf_mm(0, 8)
-            square(3)
-            spf_mm(0, 9)
-            spf_mm(0, 10)
-            h_out(1, 0, "v")
-            spf_mm(0, 11)
-            half_mm(2, [2], range(G))
-            spf_out(0, 8, "s")
-            spf_out(0, 9, "v")
-            spf_out(0, 11, "s")
-            group_h(1, "v")
+            quant_f(1, 2)
+            quant_f(2, 2)
             half_mm(2, [0], range(G))
-            spf_out(0, 10, "s")
-            h_out(2, 2, "v")
-            half_mm(2, [1], range(G))
+            h_out(1, 2, "s")
+            h_out(1, 0, "s")
+            group_h(0, "v")
             h_out(2, 0, "s")
-            quant_h(1)
+            half_mm(2, [1], range(G))
+            quant_s(0)
+            quant_h(0)
+            h_out(1, 1, "s")
+            spf_mm(0, 0)
+            spf_out(0, 0, "s")
+            spf_mm(0, 1)
+            quant_s(1)
+            spf_mm(0, 7)
+            spf_mm(0, 5)
+            spf_mm(0, 6)
+            product(8)
+            product(9)
+            spf_out(0, 1, "s")
+            spf_out(0, 6, "s")
+            product(10)
+            spf_out(0, 7, "s")
             half_mm(2, [3], range(G))
-            h_out(2, 1, "s")
-            recip(1)
-            spf_mm(1, 0)
             h_out(2, 3, "s")
-            spf_mm(1, 1)
-            spf_mm(1, 2)
-            spf_out(1, 0, "v")
-            spf_out(1, 1, "s")
+            h_out(2, 1, "s")
+            group_h(1, "v")
+            product(11)
+            quant_h(1)
+            half_mm(2, [2], range(G))
+            spf_mm(0, 4)
+            spf_out(0, 4, "s")
+            turn_s(2, 0)
+            turn_s(2, 1)
+            turned_out("s", 2, 0, "s")
+            spf_mm(0, 2)
+            spf_out(0, 5, "v")
+            turned_out("s", 2, 1, "s")
+            h_out(2, 2, "v")
+            spf_out(0, 2, "v")
+            quant_s(2)
             spf_mm(1, 3)
-            spf_mm(1, 4)
-            group_h(2, "v")
-            spf_out(1, 2, "s")
             spf_mm(1, 5)
-            spf_mm(1, 6)
+            spf_mm(1, 2)
             spf_out(1, 3, "s")
-            spf_mm(1, 7)
+            spf_out(1, 2, "s")
+            spf_mm(1, 4)
             spf_out(1, 4, "v")
-            spf_mm(1, 8)
+            turn_h(0, 0)
             spf_out(1, 5, "s")
-            turn_h(0, 1)
-            spf_out(1, 6, "v")
-            spf_out(1, 7, "s")
-            quant_h(2)
+            spf_mm(0, 3)
             spf_mm(1, 9)
-            spf_out(1, 8, "s")
-            spf_mm(1, 10)
-            turned_out("h", 0, 1, "v")
+            spf_mm(1, 8)
+            spf_out(0, 3, "v")
             spf_mm(1, 11)
-            spf_out(1, 10, "s")
-            spf_mm(2, 0)
-            spf_out(1, 9, "v")
-            spf_mm(2, 1)
-            spf_out(1, 11, "s")
-            spf_mm(2, 2)
-            spf_out(2, 0, "v")
-            turn_h(1, 0)
-            spf_out(2, 1, "s")
-            spf_out(2, 2, "v")
+            group_h(2, "v")
+            spf_mm(1, 6)
+            spf_out(1, 6, "v")
+            spf_mm(1, 10)
+            spf_mm(1, 7)
+            quant_h(2)
             turn_h(1, 1)
-            turned_out("h", 1, 0, "s")
-            quant_ht(0)
-            spf_mm(2, 3)
-            turned_out("h", 1, 1, "s")
-            recip(2)
+            turned_out("h", 0, 0, "s")
+            spf_out(1, 8, "s")
+            spf_out(1, 9, "s")
+            spf_out(1, 11, "v")
+            turn_h(1, 0)
+            spf_out(1, 7, "s")
+            spf_mm(1, 0)
+            spf_out(1, 10, "s")
+            spf_mm(1, 1)
             spf_mm(2, 4)
-            turn_h(2, 1)
-            spf_out(2, 3, "s")
-            turn_h(2, 0)
-            spf_out(2, 4, "s")
-            quant_ht(1)
+            spf_out(1, 1, "v")
+            spf_out(1, 0, "v")
             spf_mm(2, 5)
-            turned_out("h", 2, 1, "s")
-            recip(3)
-            spf_mm(2, 6)
-            turned_out("h", 2, 0, "s")
-            spf_mm(2, 7)
-            spf_mm(2, 8)
+            spf_mm(2, 1)
+            root(1)
+            spf_out(2, 4, "s")
             spf_out(2, 5, "s")
+            spf_mm(2, 0)
+            spf_mm(0, 11)
+            spf_out(2, 1, "v")
+            spf_out(2, 0, "s")
+            spf_mm(2, 6)
             spf_out(2, 6, "v")
-            spf_mm(2, 9)
-            spf_mm(2, 10)
+            turned_out("h", 1, 0, "v")
+            turned_out("h", 1, 1, "v")
+            spf_mm(2, 7)
             spf_out(2, 7, "s")
-            quant_ht(2)
+            spf_mm(2, 9)
+            spf_out(2, 9, "s")
+            side(2)
             spf_mm(2, 11)
+            spf_mm(2, 8)
             spf_out(2, 8, "s")
-            spf_out(2, 9, "v")
-            kappa_mm(0, 0)
+            spf_mm(0, 10)
+            side(1)
+            spf_out(0, 11, "s")
+            spf_mm(2, 10)
+            turn_h(2, 0)
+            turn_h(0, 1)
+            turned_out("h", 2, 0, "v")
+            turned_out("h", 0, 1, "v")
+            spf_out(0, 10, "s")
+            quant_ht(1)
+            turn_h(2, 1)
+            quant_ht(0)
             spf_out(2, 10, "s")
-            spf_out(2, 11, "v")
-            kappa_mm(0, 1)
-            kappa_out(0, 0)
+            spf_out(2, 11, "s")
+            spf_mm(0, 9)
+            turned_out("h", 2, 1, "s")
+            quant_ht(2)
             kappa_mm(1, 0)
-            kappa_out(0, 1)
+            side(0)
+            spf_mm(2, 2)
+            square(1)
+            recip(1)
+            root(3)
             kappa_mm(1, 1)
+            spf_mm(2, 3)
+            side(3)
             kappa_out(1, 0)
-            kappa_mm(2, 0)
+            square(3)
             kappa_out(1, 1)
-            kappa_mm(2, 1)
-            kappa_out(2, 0)
+            spf_out(2, 2, "s")
             kappa_mm(3, 0)
-            kappa_out(2, 1)
-            kappa_mm(3, 1)
+            recip(3)
             kappa_out(3, 0)
+            kappa_mm(3, 1)
+            root(0)
+            square(0)
+            spf_out(2, 3, "s")
+            kappa_mm(2, 0)
+            root(2)
             kappa_out(3, 1)
+            square(2)
+            kappa_mm(0, 0)
+            recip(0)
+            kappa_out(0, 0)
+            kappa_mm(0, 1)
+            kappa_out(0, 1)
+            recip(2)
+            kappa_mm(2, 1)
+            kappa_out(2, 1)
+            spf_mm(0, 8)
+            spf_out(0, 9, "s")
+            spf_out(0, 8, "s")
+            kappa_out(2, 0)

@@ -345,6 +345,7 @@ def tile_orbital_rotation_gradient_s8_kernel(
             nc.vector.memset(warm[:], 1.0)
             nc.vector.memset(cv_scales[:].rearrange("p g v -> p (g v)").bitcast(I32), 0)
             make_identity(nc, ident[:])
+            make_identity(nc, ident_b[:])
             nc.scalar.activation(out=warm[:], in_=warm[:], func=ACT.Abs_reciprocal_sqrt)
             nc.sync.dma_start(out=c_raw[0][:], in_=c_view[0])
             nc.sync.dma_start(out=scale_row[0:1, :], in_=sc_scale)
@@ -365,207 +366,222 @@ def tile_orbital_rotation_gradient_s8_kernel(
                     out=cv_scales[32 * q : 32 * q + 4, :, :].bitcast(I32),
                     in_=c_virt_scales[:, 4 * q : 4 * q + 4, :].bitcast(I32).rearrange("g q v -> q g v"),
                 )
-            group_c(1, "s")
             group_c(0, "v")
             quant_c(0)
-            group_c(2, "v")
-            quant_c(2)
-            quant_c(1)
-            nc.vector.tensor_copy(out=occ_f[:], in_=occ_b[:])
             bcast(ones_f, scale_row[:], scale_all[:])
-            bcast(ones_b, virt_row[:, NB:], virt_all[:, NB:])
-            product(0)
-            product(1)
-            bcast(ones_b, virt_row[:, :NB], virt_all[:, :NB])
-            group_f(1, 0, "v")
+            spread(("c", 1), 1)
+            spread_out(("c", 1), 1, "v")
+            spread(("c", 1), 0)
+            spread(("c", 2), 0)
+            spread_out(("c", 1), 0, "s")
+            spread(("c", 2), 1)
+            spread(("f", 0, 0), 0)
+            spread(("f", 0, 0), 1)
             product(2)
-            product(3)
-            product(6)
-            group_f(0, 0, "s")
-            group_f(2, 0, "s")
-            product(4)
-            turn_s(0, 0)
-            turn_s(0, 1)
-            turned_out("s", 0, 1, "s")
-            quant_f(1, 0)
-            turned_out("s", 0, 0, "s")
-            quant_f(0, 0)
-            quant_f(2, 0)
-            group_f(0, 2, "v")
-            half_mm(0, [3], range(G))
-            group_f(0, 1, "s")
-            half_mm(0, [1], range(G))
-            product(7)
-            half_mm(0, [2], range(G))
             product(5)
+            bcast(ones_b, virt_row[:, :NB], virt_all[:, :NB])
+            product(3)
+            bcast(ones_b, virt_row[:, NB:], virt_all[:, NB:])
+            quant_c(1)
+            product(1)
+            spread_out(("c", 2), 1, "s")
+            spread_out(("c", 2), 0, "v")
+            product(0)
+            root(2)
+            spread_out(("f", 0, 0), 0, "s")
+            spread_out(("f", 0, 0), 1, "s")
+            product(7)
+            quant_c(2)
+            nc.vector.tensor_copy(out=occ_f[:], in_=occ_b[:])
+            spread(("f", 1, 0), 0)
+            spread_out(("f", 1, 0), 0, "s")
+            turn_s(0, 1)
+            spread(("f", 2, 0), 1)
+            spread(("f", 1, 0), 1)
+            product(6)
+            turned_out("s", 0, 1, "s")
+            quant_f(0, 0)
+            spread(("f", 2, 0), 0)
+            spread_out(("f", 2, 0), 1, "s")
+            spread_out(("f", 1, 0), 1, "s")
+            product(4)
+            spread_out(("f", 2, 0), 0, "s")
+            turn_s(0, 0)
+            turned_out("s", 0, 0, "s")
+            quant_f(1, 0)
+            quant_f(2, 0)
             turn_s(1, 0)
-            group_f(1, 1, "s")
+            group_f(1, 1, "v")
+            group_f(0, 1, "s")
             quant_f(0, 1)
             group_f(1, 2, "s")
-            h_out(0, 3, "v")
-            turn_s(1, 1)
-            half_mm(0, [0], range(G))
-            h_out(0, 0, "s")
-            h_out(0, 2, "s")
-            h_out(0, 1, "s")
-            turned_out("s", 1, 1, "s")
             group_f(2, 1, "v")
+            group_f(2, 2, "s")
             quant_f(1, 1)
+            turn_s(1, 1)
+            half_mm(0, [3], range(G))
+            h_out(0, 3, "s")
+            half_mm(0, [0], range(G))
+            half_mm(0, [2], range(G))
             quant_f(2, 1)
-            turned_out("s", 1, 0, "s")
-            half_mm(1, [0], range(G))
-            half_mm(1, [2], range(G))
+            half_mm(0, [1], range(G))
+            group_f(0, 2, "v")
             half_mm(1, [3], range(G))
+            h_out(0, 0, "s")
+            half_mm(1, [0], range(G))
+            h_out(0, 1, "s")
             half_mm(1, [1], range(G))
-            group_f(2, 2, "v")
-            quant_f(0, 2)
-            h_out(1, 3, "s")
+            h_out(0, 2, "s")
             quant_f(1, 2)
+            half_mm(1, [2], range(G))
             quant_f(2, 2)
-            half_mm(2, [0], range(G))
-            h_out(1, 2, "s")
-            h_out(1, 0, "s")
-            group_h(0, "v")
-            h_out(2, 0, "s")
+            quant_f(0, 2)
             half_mm(2, [1], range(G))
+            group_h(0, "v")
             quant_s(0)
+            h_out(1, 3, "s")
             quant_h(0)
+            product(9)
+            turned_out("s", 1, 1, "s")
+            h_out(1, 0, "s")
             h_out(1, 1, "s")
+            half_mm(2, [3], range(G))
+            h_out(1, 2, "s")
+            product(8)
+            turned_out("s", 1, 0, "s")
+            product(11)
+            h_out(2, 1, "s")
+            spf_mm(0, 2)
+            product(10)
+            spf_mm(0, 3)
+            spf_out(0, 2, "s")
+            spf_out(0, 3, "s")
             spf_mm(0, 0)
             spf_out(0, 0, "s")
             spf_mm(0, 1)
-            quant_s(1)
-            spf_mm(0, 7)
-            spf_mm(0, 5)
-            spf_mm(0, 6)
-            product(8)
-            product(9)
             spf_out(0, 1, "s")
-            spf_out(0, 6, "s")
-            product(10)
-            spf_out(0, 7, "s")
-            half_mm(2, [3], range(G))
-            h_out(2, 3, "s")
-            h_out(2, 1, "s")
-            group_h(1, "v")
-            product(11)
-            quant_h(1)
             half_mm(2, [2], range(G))
-            spf_mm(0, 4)
-            spf_out(0, 4, "s")
+            h_out(2, 2, "s")
             turn_s(2, 0)
             turn_s(2, 1)
             turned_out("s", 2, 0, "s")
-            spf_mm(0, 2)
-            spf_out(0, 5, "v")
+            h_out(2, 3, "s")
+            quant_s(1)
+            spf_mm(0, 7)
+            spf_mm(0, 6)
+            group_h(1, "v")
+            spf_out(0, 7, "v")
+            half_mm(2, [0], range(G))
             turned_out("s", 2, 1, "s")
-            h_out(2, 2, "v")
-            spf_out(0, 2, "v")
-            quant_s(2)
-            spf_mm(1, 3)
-            spf_mm(1, 5)
-            spf_mm(1, 2)
-            spf_out(1, 3, "s")
-            spf_out(1, 2, "s")
-            spf_mm(1, 4)
-            spf_out(1, 4, "v")
             turn_h(0, 0)
-            spf_out(1, 5, "s")
-            spf_mm(0, 3)
-            spf_mm(1, 9)
-            spf_mm(1, 8)
-            spf_out(0, 3, "v")
-            spf_mm(1, 11)
-            group_h(2, "v")
-            spf_mm(1, 6)
-            spf_out(1, 6, "v")
-            spf_mm(1, 10)
-            spf_mm(1, 7)
-            quant_h(2)
-            turn_h(1, 1)
-            turned_out("h", 0, 0, "s")
-            spf_out(1, 8, "s")
-            spf_out(1, 9, "s")
-            spf_out(1, 11, "v")
-            turn_h(1, 0)
-            spf_out(1, 7, "s")
-            spf_mm(1, 0)
-            spf_out(1, 10, "s")
+            turn_h(2, 1)
+            spf_out(0, 6, "s")
+            quant_h(1)
             spf_mm(1, 1)
-            spf_mm(2, 4)
-            spf_out(1, 1, "v")
-            spf_out(1, 0, "v")
-            spf_mm(2, 5)
-            spf_mm(2, 1)
-            root(1)
-            spf_out(2, 4, "s")
-            spf_out(2, 5, "s")
-            spf_mm(2, 0)
+            square(2)
+            h_out(2, 0, "v")
+            spf_mm(1, 0)
+            spf_mm(1, 5)
+            spf_mm(1, 4)
+            quant_s(2)
+            spf_mm(1, 11)
+            spf_out(1, 1, "s")
+            spf_mm(0, 10)
+            spf_out(1, 0, "s")
+            spf_out(1, 5, "s")
+            spf_out(1, 4, "s")
+            spf_mm(1, 10)
+            spf_out(1, 10, "s")
             spf_mm(0, 11)
-            spf_out(2, 1, "v")
-            spf_out(2, 0, "s")
+            spf_out(0, 11, "s")
+            group_h(2, "v")
+            spf_out(1, 11, "v")
+            quant_h(2)
+            spf_out(0, 10, "v")
+            spf_mm(0, 9)
+            spf_out(0, 9, "s")
+            spf_mm(0, 8)
+            spf_mm(1, 3)
+            spf_out(1, 3, "s")
+            spf_out(0, 8, "v")
+            spf_mm(1, 2)
+            spf_out(1, 2, "v")
+            spf_mm(1, 7)
             spf_mm(2, 6)
+            turned_out("h", 2, 1, "s")
             spf_out(2, 6, "v")
-            turned_out("h", 1, 0, "v")
-            turned_out("h", 1, 1, "v")
+            turned_out("h", 0, 0, "s")
+            spf_mm(2, 3)
             spf_mm(2, 7)
+            spf_mm(2, 2)
+            turn_h(1, 0)
+            spf_out(2, 3, "v")
             spf_out(2, 7, "s")
+            turn_h(1, 1)
+            spf_out(1, 7, "s")
+            side(0)
+            spf_mm(1, 6)
+            turned_out("h", 1, 1, "s")
+            turned_out("h", 1, 0, "v")
+            spf_out(1, 6, "s")
+            spf_out(2, 2, "v")
+            turn_h(0, 1)
+            side(2)
+            root(0)
+            turn_h(2, 0)
+            turned_out("h", 2, 0, "s")
+            spf_mm(2, 4)
+            spf_out(2, 4, "s")
+            spf_mm(2, 5)
+            spf_out(2, 5, "s")
+            turned_out("h", 0, 1, "v")
+            spf_mm(1, 8)
             spf_mm(2, 9)
             spf_out(2, 9, "s")
-            side(2)
-            spf_mm(2, 11)
             spf_mm(2, 8)
             spf_out(2, 8, "s")
-            spf_mm(0, 10)
-            side(1)
-            spf_out(0, 11, "s")
-            spf_mm(2, 10)
-            turn_h(2, 0)
-            turn_h(0, 1)
-            turned_out("h", 2, 0, "v")
-            turned_out("h", 0, 1, "v")
-            spf_out(0, 10, "s")
+            square(0)
             quant_ht(1)
-            turn_h(2, 1)
+            spf_mm(0, 5)
+            spf_out(1, 8, "s")
             quant_ht(0)
-            spf_out(2, 10, "s")
-            spf_out(2, 11, "s")
-            spf_mm(0, 9)
-            turned_out("h", 2, 1, "s")
+            spf_mm(1, 9)
             quant_ht(2)
-            kappa_mm(1, 0)
-            side(0)
-            spf_mm(2, 2)
+            spf_out(1, 9, "s")
+            kappa_mm(2, 1)
+            recip(2)
+            kappa_mm(2, 0)
+            side(1)
+            kappa_out(2, 1)
+            kappa_mm(0, 1)
+            recip(0)
+            root(1)
             square(1)
+            kappa_out(2, 0)
+            kappa_mm(0, 0)
+            spf_mm(0, 4)
+            kappa_out(0, 1)
+            kappa_out(0, 0)
+            spf_mm(2, 1)
+            spf_out(0, 5, "s")
             recip(1)
+            spf_out(0, 4, "s")
+            kappa_mm(1, 0)
             root(3)
-            kappa_mm(1, 1)
-            spf_mm(2, 3)
-            side(3)
-            kappa_out(1, 0)
             square(3)
+            kappa_mm(1, 1)
+            spf_mm(2, 0)
+            side(3)
+            spf_out(2, 1, "s")
+            kappa_out(1, 0)
+            spf_mm(2, 11)
+            spf_out(2, 0, "s")
+            spf_mm(2, 10)
+            kappa_mm(3, 1)
             kappa_out(1, 1)
-            spf_out(2, 2, "s")
             kappa_mm(3, 0)
             recip(3)
-            kappa_out(3, 0)
-            kappa_mm(3, 1)
-            root(0)
-            square(0)
-            spf_out(2, 3, "s")
-            kappa_mm(2, 0)
-            root(2)
             kappa_out(3, 1)
-            square(2)
-            kappa_mm(0, 0)
-            recip(0)
-            kappa_out(0, 0)
-            kappa_mm(0, 1)
-            kappa_out(0, 1)
-            recip(2)
-            kappa_mm(2, 1)
-            kappa_out(2, 1)
-            spf_mm(0, 8)
-            spf_out(0, 9, "s")
-            spf_out(0, 8, "s")
-            kappa_out(2, 0)
+            spf_out(2, 11, "s")
+            spf_out(2, 10, "s")
+            kappa_out(3, 0)

@@ -17,9 +17,11 @@ ALU = mybir.AluOpType
 P = 128
 PACK = 4
 B, O, V = 1536, 512, 1024
-G = B // 512
-NB = 512
-RT = B // P
+COLS = 512
+G = B // (P * PACK)
+ROWS = B // P
+HALF_ROWS = ROWS // 2
+
 FLOPS = 2 * O * B * B + 2 * O * B * V + 2 * B * O * B
 
 
@@ -30,7 +32,7 @@ def tile_orbital_rotation_gradient_s8_kernel(
     with ExitStack() as ctx:
         keep = ctx.enter_context(tc.tile_pool(name="keep", bufs=1))
         work = ctx.enter_context(tc.tile_pool(name="work", bufs=3))
-        outs = ctx.enter_context(tc.tile_pool(name="outs", bufs=12))
+        big = ctx.enter_context(tc.tile_pool(name="big", bufs=12))
         mm = ctx.enter_context(tc.psum_pool(name="mm", bufs=6))
         tr = ctx.enter_context(tc.psum_pool(name="tr", bufs=2))
 
@@ -39,27 +41,23 @@ def tile_orbital_rotation_gradient_s8_kernel(
         ones_f = keep.tile([P, P], F32, name="ones_f")
         ones_b = keep.tile([P, P], BF16, name="ones_b")
         ident = keep.tile([P, P], F32, name="ident")
-        occ_b = keep.tile([P, PACK], BF16, name="occ_b")
-        eocc_b = keep.tile([P, PACK], BF16, name="eocc_b")
-        occ_f = keep.tile([P, PACK], F32, name="occ_f")
-        eocc_f = keep.tile([P, PACK], F32, name="eocc_f")
         scale_all = keep.tile([P, O], F32, name="scale_all")
         virt_all = keep.tile([P, V], BF16, name="virt_all")
-        below = keep.tile([P, PACK, V], BF16, name="below")
-        ident_b = keep.tile([P, P], BF16, name="ident_b")
-        rgap = keep.tile([P, PACK, V], F32, name="rgap")
-        warm = keep.tile([P, 1], F32, name="warm")
-        c_raw = [outs.tile([P, PACK, O], BF16, name="staged") for g in range(G)]
-        f_raw0 = [outs.tile([P, PACK, NB], BF16, name="staged") for g in range(G)]
-        f_raw1 = [keep.tile([P, PACK, 2 * NB], BF16, name=f"f_raw1_{g}") for g in range(G)]
-        sc_raw = [keep.tile([P, RT // 2, O], U8, name=f"sc_raw{h}") for h in range(2)]
+        per_orbital_b = keep.tile([P, 2, 16], BF16, name="per_orbital_b")
+        per_orbital = keep.tile([P, 2, PACK], F32, name="per_orbital")
+        first_function = keep.tile([P, 1], F32, name="first_function")
+
+        c_raw = [big.tile([P, PACK, O], BF16, name="big4k") for g in range(G)]
+        f_raw_first = [big.tile([P, PACK, COLS], BF16, name="big4k") for g in range(G)]
+        f_raw_rest = [keep.tile([P, PACK, B - COLS], BF16, name=f"f_raw_rest{g}") for g in range(G)]
+        s_raw = [keep.tile([P, HALF_ROWS, O], U8, name=f"s_raw{k}") for k in range(2)]
         cv_words = keep.tile([P, G, 2 * V], U8, name="cv_words", align_bytes=64)
         cv_scales = keep.tile([P, G, V], U8, name="cv_scales", align_bytes=64)
+
         c_codes = keep.tile([P, G, O], U32, name="c_codes", align_bytes=64)
         c_scales = keep.tile([P, G, O], U8, name="c_scales", align_bytes=64)
         f_codes = keep.tile([P, G, B], U32, name="f_codes", align_bytes=64)
         f_scales = keep.tile([P, G, B], U8, name="f_scales", align_bytes=64)
-        h_bf = keep.tile([P, PACK, B], BF16, name="h_bf", align_bytes=64)
         h_codes = keep.tile([P, B], U32, name="h_codes", align_bytes=64)
         h_scales = keep.tile([P, B], U8, name="h_scales", align_bytes=64)
         ht_codes = keep.tile([P, G, O], U32, name="ht_codes", align_bytes=64)
@@ -67,11 +65,18 @@ def tile_orbital_rotation_gradient_s8_kernel(
         s_codes = keep.tile([P, B], U32, name="s_codes", align_bytes=64)
         s_scales = keep.tile([P, B], U8, name="s_scales", align_bytes=64)
 
+        h_bf = keep.tile([P, PACK, B], BF16, name="h_bf", align_bytes=64)
+        below = keep.tile([P, PACK, V], BF16, name="below")
+        rgap = keep.tile([P, PACK, V], F32, name="rgap")
+
         c_view = c_occ.rearrange("(g p j) o -> g p j o", p=P, j=PACK)
         f_view = fock.rearrange("(g p j) n -> g p j n", p=P, j=PACK)
-        sc_view = sc_bytes.rearrange("(p i) o -> p i o", i=RT)
-        spf_view = spf.rearrange("(p i) n -> p i n", i=RT)
+        s_view = sc_bytes.rearrange("(p i) o -> p i o", i=ROWS)
+        spf_view = spf.rearrange("(p i) n -> p i n", i=ROWS)
         kappa_view = kappa.rearrange("(p t) v -> p t v", t=PACK)
+
+        def block(n):
+            return slice(n * COLS, (n + 1) * COLS)
 
         def copy(engine, out, in_):
             if engine == "v":
@@ -79,509 +84,421 @@ def tile_orbital_rotation_gradient_s8_kernel(
             else:
                 nc.scalar.copy(out=out, in_=in_)
 
-        grouped = {}
-
-        def new_grouped(key):
-            t = work.tile([P, NB, PACK], BF16, name="grouped", align_bytes=64, bufs=5)
-            grouped[key] = t
-            return t
-
-        def flat(key):
-            return grouped[key][:].rearrange("p c t -> p (c t)")
-
-        spread_ps = {}
-
-        def raw_view(key):
-            if key[0] == "c":
-                return c_raw[key[1]][:].rearrange("p j (m t) -> p t m j", t=PACK)
-            g, n = key[1:]
-            src = f_raw0[g][:] if n == 0 else f_raw1[g][:, :, (n - 1) * NB : n * NB]
-            return src.rearrange("p j (t m) -> p t m j", t=PACK)
-
-        def spread(key, half):
-            ps = mm.tile([P, 2 * NB], BF16, name="ps")
-            spread_ps[key, half] = ps
-            for k in range(2):
-                nc.tensor.matmul(
-                    out=ps[:, k * NB : (k + 1) * NB].rearrange("p (c t) -> p c t", t=PACK),
-                    lhsT=ident_b[:],
-                    rhs=raw_view(key)[:, 2 * half + k, :, :],
-                    start=True,
-                    stop=True,
-                )
-
-        def spread_out(key, half, engine):
-            if key not in grouped:
-                new_grouped(key)
-            copy(
-                engine,
-                grouped[key][:, half * 256 : (half + 1) * 256, :].rearrange("p c t -> p (c t)"),
-                spread_ps[key, half][:],
+        def quantize(source, codes, scales):
+            nc.vector.quantize_mx(
+                out=codes.bitcast(FP8X4), scales=scales, in_=source[:].rearrange("p c j -> p (c j)")
             )
 
-        def group_c(g, engine):
-            dst = new_grouped(("c", g))
+        def broadcast_scale():
+            ps = mm.tile([P, COLS], F32, name="ps")
+            nc.tensor.matmul(out=ps[:], lhsT=ones_f[:], rhs=scale_row[:], start=True, stop=True)
+            nc.scalar.copy(out=scale_all[:], in_=ps[:])
+
+        def broadcast_virt(v):
+            ps = mm.tile([P, COLS], F32, name="ps")
+            nc.tensor.matmul(out=ps[:], lhsT=ones_b[:], rhs=virt_row[:, block(v)], start=True, stop=True)
+            nc.scalar.copy(out=virt_all[:, block(v)], in_=ps[:])
+
+        interleaved = {}
+
+        def new_interleaved(key):
+            tile = work.tile([P, COLS, PACK], BF16, name="interleaved", align_bytes=64, bufs=5)
+            interleaved[key] = tile
+            return tile
+
+        def interleave_by_four(tile, source, engine):
             copy(
                 engine,
-                dst[:].rearrange("p (t m) j -> p t m j", t=PACK),
+                tile[:].rearrange("p (c i) j -> p c j i", i=4),
+                source.rearrange("p j (c i) -> p c j i", i=4),
+            )
+
+        def interleave_c(g, engine):
+            copy(
+                engine,
+                new_interleaved(("c", g))[:].rearrange("p (t m) j -> p t m j", t=PACK),
                 c_raw[g][:].rearrange("p j (m t) -> p t m j", t=PACK),
             )
 
-        def quant_c(g):
-            nc.vector.quantize_mx(
-                out=c_codes[:, g, :].bitcast(FP8X4), scales=c_scales[:, g, :], in_=flat(("c", g))
-            )
+        def quantize_c(g):
+            quantize(interleaved["c", g], c_codes[:, g, :], c_scales[:, g, :])
 
-        def group_f(g, n, engine):
-            dst = new_grouped(("f", g, n))
-            src = f_raw0[g][:] if n == 0 else f_raw1[g][:, :, (n - 1) * NB : n * NB]
-            copy(
-                engine,
-                dst[:].rearrange("p (c i) t -> p c t i", i=4),
-                src.rearrange("p t (c i) -> p c t i", i=4),
-            )
+        def interleave_f(n, g, engine):
+            source = f_raw_first[g][:] if n == 0 else f_raw_rest[g][:, :, block(n - 1)]
+            interleave_by_four(new_interleaved(("f", n, g)), source, engine)
 
-        def quant_f(g, n):
-            cols = slice(n * NB, (n + 1) * NB)
-            nc.vector.quantize_mx(
-                out=f_codes[:, g, cols].bitcast(FP8X4), scales=f_scales[:, g, cols], in_=flat(("f", g, n))
-            )
+        def quantize_f(n, g):
+            quantize(interleaved["f", n, g], f_codes[:, g, block(n)], f_scales[:, g, block(n)])
+
+        def interleave_h(n, engine):
+            interleave_by_four(new_interleaved(("h", n)), h_bf[:, :, block(n)], engine)
+
+        def quantize_h(n):
+            quantize(interleaved["h", n], h_codes[:, block(n)], h_scales[:, block(n)])
 
         half = {}
 
-        def half_mm(n, tiles, groups):
-            cols = slice(n * NB, (n + 1) * NB)
-            for t in tiles:
-                for g in groups:
-                    if g == 0:
-                        ps = mm.tile([P, NB], F32, name="ps")
-                        half[n, t] = ps
-                    nc.tensor.matmul_mx(
-                        out=half[n, t][:],
-                        lhsT=c_codes[:, g, t * P : (t + 1) * P].bitcast(FP8X4),
-                        lhsT_scale=c_scales[:, g, t * P : (t + 1) * P],
-                        rhs=f_codes[:, g, cols].bitcast(FP8X4),
-                        rhs_scale=f_scales[:, g, cols],
-                        start=(g == 0),
-                        stop=(g == G - 1),
-                    )
+        def half_mm(n, t):
+            ps = mm.tile([P, COLS], F32, name="ps")
+            half[n, t] = ps
+            orbitals = slice(t * P, (t + 1) * P)
+            for g in range(G):
+                nc.tensor.matmul_mx(
+                    out=ps[:],
+                    lhsT=c_codes[:, g, orbitals].bitcast(FP8X4),
+                    lhsT_scale=c_scales[:, g, orbitals],
+                    rhs=f_codes[:, g, block(n)].bitcast(FP8X4),
+                    rhs_scale=f_scales[:, g, block(n)],
+                    start=(g == 0),
+                    stop=(g == G - 1),
+                )
 
         def h_out(n, t, engine):
-            cols = slice(n * NB, (n + 1) * NB)
+            out, factor = h_bf[:, t, block(n)], per_orbital[:, 0, t : t + 1]
             if engine == "v":
-                nc.vector.tensor_scalar(
-                    out=h_bf[:, t, cols], in0=half[n, t][:], scalar1=occ_f[:, t : t + 1], scalar2=None, op0=ALU.mult
-                )
+                nc.vector.tensor_scalar(out=out, in0=half[n, t][:], scalar1=factor, scalar2=None, op0=ALU.mult)
             else:
-                nc.scalar.activation(
-                    out=h_bf[:, t, cols], in_=half[n, t][:], func=ACT.Copy, scale=occ_f[:, t : t + 1]
-                )
+                nc.scalar.activation(out=out, in_=half[n, t][:], func=ACT.Copy, scale=factor)
 
-        def group_h(n, engine):
-            dst = new_grouped(("h", n))
+        in_psum, turned = {}, {}
+
+        def turn(key, rows):
+            ps = tr.tile([P, 4, P], F32, name="pt")
+            in_psum[key] = ps
+            for k in range(2):
+                words = rows[k].bitcast(F32)
+                for u in range(2):
+                    nc.tensor.transpose(ps[:, 2 * k + u, :], words[:, u : COLS // 2 : 2], ident[:])
+
+        def turned_out(key, engine):
+            what, pair = key[:2], key[2]
+            if what not in turned:
+                tile = work.tile([P, COLS, PACK], BF16, name="turned", align_bytes=64, bufs=4)
+                turned[what] = tile
+            words = turned[what][:].rearrange("p c j -> p (c j)").bitcast(F32)
             copy(
                 engine,
-                dst[:].rearrange("p (c i) t -> p c t i", i=4),
-                h_bf[:, :, n * NB : (n + 1) * NB].rearrange("p t (c i) -> p c t i", i=4),
+                words[:, block(pair)].rearrange("p (k r u) -> p k r u", k=2, u=2),
+                in_psum[key][:].rearrange("p (k u) r -> p k r u", k=2),
             )
-
-        def quant_h(n):
-            cols = slice(n * NB, (n + 1) * NB)
-            nc.vector.quantize_mx(
-                out=h_codes[:, cols].bitcast(FP8X4), scales=h_scales[:, cols], in_=flat(("h", n))
-            )
-
-        turned = {}
 
         def turn_h(n, pair):
-            ps = tr.tile([P, 4, P], F32, name="pt")
-            turned["h", n, pair] = ps
-            for k in range(2):
-                words = h_bf[:, 2 * pair + k, n * NB : (n + 1) * NB].bitcast(F32)
-                for u in range(2):
-                    nc.tensor.transpose(ps[:, 2 * k + u, :], words[:, u : NB // 2 : 2], ident[:])
+            turn(("h", n, pair), [h_bf[:, 2 * pair + k, block(n)] for k in range(2)])
 
-        def turned_out(what, n, pair, engine):
-            key = (what + "t", n)
-            if key not in grouped:
-                t = work.tile([P, NB, PACK], BF16, name="turned_sb", align_bytes=64, bufs=4)
-                grouped[key] = t
-            words = grouped[key][:].rearrange("p c t -> p (c t)").bitcast(F32)
-            copy(
-                engine,
-                words[:, pair * NB : (pair + 1) * NB].rearrange("p (k r u) -> p k r u", k=2, u=2),
-                turned[what, n, pair][:].rearrange("p (k u) r -> p k r u", k=2),
-            )
+        def turned_h_out(n, pair, engine):
+            turned_out(("h", n, pair), engine)
 
-        def quant_ht(n):
-            nc.vector.quantize_mx(
-                out=ht_codes[:, n, :].bitcast(FP8X4), scales=ht_scales[:, n, :], in_=flat(("ht", n))
-            )
+        def quantize_ht(n):
+            quantize(turned["h", n], ht_codes[:, n, :], ht_scales[:, n, :])
 
-        sc_bf = {}
+        s_bf = {}
 
-        def product(i):
-            if i // 4 not in sc_bf:
-                t = work.tile([P, 4, O], BF16, name="sc_bf", bufs=3)
-                sc_bf[i // 4] = t
+        def widen_s(i):
+            if i // 4 not in s_bf:
+                tile = work.tile([P, 4, O], BF16, name="s_bf")
+                s_bf[i // 4] = tile
             nc.vector.tensor_tensor(
-                out=sc_bf[i // 4][:, i % 4, :],
-                in0=sc_raw[i // (RT // 2)][:, i % (RT // 2), :].bitcast(FP8),
+                out=s_bf[i // 4][:, i % 4, :],
+                in0=s_raw[i // HALF_ROWS][:, i % HALF_ROWS, :].bitcast(FP8),
                 in1=scale_all[:],
                 op=ALU.mult,
             )
 
-        def turn_s(c, pair):
-            ps = tr.tile([P, 4, P], F32, name="pt")
-            turned["s", c, pair] = ps
-            for k in range(2):
-                words = sc_bf[c][:, 2 * pair + k, :].bitcast(F32)
-                for u in range(2):
-                    nc.tensor.transpose(ps[:, 2 * k + u, :], words[:, u : O // 2 : 2], ident[:])
+        def turn_s(chunk, pair):
+            turn(("s", chunk, pair), [s_bf[chunk][:, 2 * pair + k, :] for k in range(2)])
 
-        def quant_s(c):
-            cols = slice(c * NB, (c + 1) * NB)
-            nc.vector.quantize_mx(
-                out=s_codes[:, cols].bitcast(FP8X4), scales=s_scales[:, cols], in_=flat(("st", c))
-            )
+        def turned_s_out(chunk, pair, engine):
+            turned_out(("s", chunk, pair), engine)
 
-        prod = {}
+        def quantize_s(chunk):
+            quantize(turned["s", chunk], s_codes[:, block(chunk)], s_scales[:, block(chunk)])
+
+        product, result = {}, {}
 
         def spf_mm(n, i):
-            ps = mm.tile([P, NB], F32, name="ps")
-            prod[n, i] = ps
-            cols = slice(n * NB, (n + 1) * NB)
+            ps = mm.tile([P, COLS], F32, name="ps")
+            product[n, i] = ps
+            rows = slice(i * P, (i + 1) * P)
             nc.tensor.matmul_mx(
                 out=ps[:],
-                lhsT=s_codes[:, i * P : (i + 1) * P].bitcast(FP8X4),
-                lhsT_scale=s_scales[:, i * P : (i + 1) * P],
-                rhs=h_codes[:, cols].bitcast(FP8X4),
-                rhs_scale=h_scales[:, cols],
+                lhsT=s_codes[:, rows].bitcast(FP8X4),
+                lhsT_scale=s_scales[:, rows],
+                rhs=h_codes[:, block(n)].bitcast(FP8X4),
+                rhs_scale=h_scales[:, block(n)],
                 start=True,
                 stop=True,
             )
 
-        staged = {}
-
         def spf_out(n, i, engine):
-            first = (n, i // 2) not in staged
-            if first:
-                t = outs.tile([P, 2, NB], F32, name="staged")
-                staged[n, i // 2] = t
-            copy(engine, staged[n, i // 2][:, i % 2, :], prod[n, i][:])
-            if not first:
-                spf_store(n, i // 2)
+            pair = (n, i // 2)
+            if pair not in result:
+                tile = big.tile([P, 2, COLS], F32, name="big4k")
+                result[pair] = tile
+            copy(engine, result[pair][:, i % 2, :], product[n, i][:])
+            if i % 2:
+                nc.sync.dma_start(out=spf_view[:, i - 1 : i + 1, block(n)], in_=result[pair][:])
 
-        def spf_store(n, j):
-            nc.sync.dma_start(
-                out=spf_view[:, 2 * j : 2 * j + 2, n * NB : (n + 1) * NB], in_=staged[n, j][:]
+        def gap_root(t):
+            nc.scalar.activation(
+                out=rgap[:, t, :],
+                in_=virt_all[:],
+                func=ACT.Abs_reciprocal_sqrt,
+                scale=-1.0,
+                bias=per_orbital[:, 1, t : t + 1],
+            )
+
+        def gap_square(t):
+            nc.scalar.activation(out=rgap[:, t, :], in_=rgap[:, t, :], func=ACT.Square)
+
+        def gap_side(t):
+            nc.vector.tensor_scalar(
+                out=below[:, t, :],
+                in0=virt_all[:],
+                scalar1=per_orbital[:, 1, t : t + 1],
+                scalar2=2.0,
+                op0=ALU.is_lt,
+                op1=ALU.mult,
+            )
+
+        def gap_sign(t):
+            nc.vector.scalar_tensor_tensor(
+                out=rgap[:, t, :], in0=below[:, t, :], scalar=1.0, in1=rgap[:, t, :], op0=ALU.subtract, op1=ALU.mult
             )
 
         grad = {}
 
         def kappa_mm(t, v):
-            ps = mm.tile([P, NB], F32, name="ps")
+            ps = mm.tile([P, COLS], F32, name="ps")
             grad[t, v] = ps
+            orbitals = slice(t * P, (t + 1) * P)
             for g in range(G):
                 nc.tensor.matmul_mx(
                     out=ps[:],
-                    lhsT=ht_codes[:, g, t * P : (t + 1) * P].bitcast(FP8X4),
-                    lhsT_scale=ht_scales[:, g, t * P : (t + 1) * P],
-                    rhs=cv_words[:, g, 2 * NB * v : 2 * NB * (v + 1)].bitcast(FP4X4),
-                    rhs_scale=cv_scales[:, g, NB * v : NB * (v + 1)],
+                    lhsT=ht_codes[:, g, orbitals].bitcast(FP8X4),
+                    lhsT_scale=ht_scales[:, g, orbitals],
+                    rhs=cv_words[:, g, 2 * COLS * v : 2 * COLS * (v + 1)].bitcast(FP4X4),
+                    rhs_scale=cv_scales[:, g, block(v)],
                     start=(g == 0),
                     stop=(g == G - 1),
                 )
 
-        kappa_done = {}
-
         def kappa_out(t, v):
-            cols = slice(v * NB, (v + 1) * NB)
-            nc.vector.tensor_tensor(out=rgap[:, t, cols], in0=grad[t, v][:], in1=rgap[:, t, cols], op=ALU.mult)
-            if t in kappa_done:
-                kappa_store(t)
-            kappa_done[t] = v
-
-        def kappa_store(t):
-            nc.sync.dma_start(out=kappa_view[:, t, :], in_=rgap[:, t, :])
-
-
-        def bcast(ones, row, dst):
-            ps = mm.tile([P, NB], F32, name="ps")
-            nc.tensor.matmul(out=ps[:], lhsT=ones[:], rhs=row, start=True, stop=True)
-            nc.scalar.copy(out=dst, in_=ps[:])
-
-        def recip(t):
-            nc.vector.scalar_tensor_tensor(
-                out=rgap[:, t, :], in0=below[:, t, :], scalar=1.0, in1=rgap[:, t, :], op0=ALU.subtract, op1=ALU.mult
+            nc.vector.tensor_tensor(
+                out=rgap[:, t, block(v)], in0=grad[t, v][:], in1=rgap[:, t, block(v)], op=ALU.mult
             )
-
-        def side(t):
-            nc.vector.tensor_scalar(
-                out=below[:, t, :], in0=virt_all[:], scalar1=eocc_b[:, t : t + 1], scalar2=2.0, op0=ALU.is_lt, op1=ALU.mult
-            )
-
-        def root(t):
-            nc.scalar.activation(
-                out=rgap[:, t, :], in_=virt_all[:], func=ACT.Abs_reciprocal_sqrt, scale=-1.0, bias=eocc_b[:, t : t + 1]
-            )
-
-        def square(t):
-            nc.scalar.activation(out=rgap[:, t, :], in_=rgap[:, t, :], func=ACT.Square)
-
-        def spf_tile(n, i, engine):
-            spf_mm(n, i)
-            spf_out(n, i, engine)
-
-        def product_run(*rows):
-            for i in rows:
-                product(i)
+            if t == PACK - 1:
+                nc.sync.dma_start(out=kappa_view[:, t, block(v)], in_=rgap[:, t, block(v)])
+            elif v == 1:
+                nc.sync.dma_start(out=kappa_view[:, t, :], in_=rgap[:, t, :])
 
         with tc.manual_schedule():
             nc.vector.memset(scale_row[:], 0.0)
             nc.vector.memset(ones_f[:], 1.0)
             nc.vector.memset(virt_row[:], 0.0)
             nc.vector.memset(ones_b[:], 1.0)
-            nc.vector.memset(warm[:], 1.0)
+            nc.vector.memset(first_function[:], 1.0)
             nc.vector.memset(cv_scales[:].rearrange("p g v -> p (g v)").bitcast(I32), 0)
             make_identity(nc, ident[:])
-            make_identity(nc, ident_b[:])
-            nc.scalar.activation(out=warm[:], in_=warm[:], func=ACT.Abs_reciprocal_sqrt)
+            nc.scalar.activation(out=first_function[:], in_=first_function[:], func=ACT.Abs_reciprocal_sqrt)
+
             nc.sync.dma_start(out=c_raw[0][:], in_=c_view[0])
             nc.sync.dma_start(out=scale_row[0:1, :], in_=sc_scale)
             nc.sync.dma_start(out=virt_row[0:1, :], in_=e_virt.rearrange("(o v) -> o v", o=1))
-            nc.sync.dma_start(out=eocc_b[:], in_=e_occ.rearrange("(p t) -> p t", t=PACK))
-            nc.sync.dma_start(out=occ_b[:], in_=occ.rearrange("(p t) -> p t", t=PACK))
-            nc.sync.dma_start(out=c_raw[1][:], in_=c_view[1])
-            nc.sync.dma_start(out=c_raw[2][:], in_=c_view[2])
-            nc.sync.dma_start(out=sc_raw[0][:], in_=sc_view[:, : RT // 2, :])
+            nc.sync.dma_start(out=per_orbital_b[:, 1, :PACK], in_=e_occ.rearrange("(p t) -> p t", t=PACK))
+            nc.sync.dma_start(out=per_orbital_b[:, 0, :PACK], in_=occ.rearrange("(p t) -> p t", t=PACK))
+            for g in range(1, G):
+                nc.sync.dma_start(out=c_raw[g][:], in_=c_view[g])
+            nc.sync.dma_start(out=s_raw[0][:], in_=s_view[:, :HALF_ROWS, :])
             for g in range(G):
-                nc.sync.dma_start(out=f_raw0[g][:], in_=f_view[g, :, :, :NB])
-            nc.sync.dma_start(out=sc_raw[1][:], in_=sc_view[:, RT // 2 :, :])
+                nc.sync.dma_start(out=f_raw_first[g][:], in_=f_view[g, :, :, :COLS])
+            nc.sync.dma_start(out=s_raw[1][:], in_=s_view[:, HALF_ROWS:, :])
             for g in range(G):
-                nc.sync.dma_start(out=f_raw1[g][:], in_=f_view[g, :, :, NB:])
+                nc.sync.dma_start(out=f_raw_rest[g][:], in_=f_view[g, :, :, COLS:])
             nc.sync.dma_start(out=cv_words[:], in_=c_virt_words.rearrange("g p n -> p g n"))
             for q in range(4):
                 nc.sync.dma_start(
                     out=cv_scales[32 * q : 32 * q + 4, :, :].bitcast(I32),
                     in_=c_virt_scales[:, 4 * q : 4 * q + 4, :].bitcast(I32).rearrange("g q v -> q g v"),
                 )
-            group_c(0, "v")
-            quant_c(0)
-            bcast(ones_f, scale_row[:], scale_all[:])
-            spread(("c", 1), 1)
-            spread_out(("c", 1), 1, "v")
-            spread(("c", 1), 0)
-            spread(("c", 2), 0)
-            spread_out(("c", 1), 0, "s")
-            spread(("c", 2), 1)
-            spread(("f", 0, 0), 0)
-            spread(("f", 0, 0), 1)
-            product(2)
-            product(5)
-            bcast(ones_b, virt_row[:, :NB], virt_all[:, :NB])
-            product(3)
-            bcast(ones_b, virt_row[:, NB:], virt_all[:, NB:])
-            quant_c(1)
-            product(1)
-            spread_out(("c", 2), 1, "s")
-            spread_out(("c", 2), 0, "v")
-            product(0)
-            root(2)
-            spread_out(("f", 0, 0), 0, "s")
-            spread_out(("f", 0, 0), 1, "s")
-            product(7)
-            quant_c(2)
-            nc.vector.tensor_copy(out=occ_f[:], in_=occ_b[:])
-            spread(("f", 1, 0), 0)
-            spread_out(("f", 1, 0), 0, "s")
-            turn_s(0, 1)
-            spread(("f", 2, 0), 1)
-            spread(("f", 1, 0), 1)
-            product(6)
-            turned_out("s", 0, 1, "s")
-            quant_f(0, 0)
-            spread(("f", 2, 0), 0)
-            spread_out(("f", 2, 0), 1, "s")
-            spread_out(("f", 1, 0), 1, "s")
-            product(4)
-            spread_out(("f", 2, 0), 0, "s")
-            turn_s(0, 0)
-            turned_out("s", 0, 0, "s")
-            quant_f(1, 0)
-            quant_f(2, 0)
+
+            interleave_c(0, "v")
+            nc.vector.tensor_copy(out=per_orbital[:], in_=per_orbital_b[:, :, :PACK])
+            broadcast_virt(0)
+            interleave_c(1, "s")
+            quantize_c(0)
+            interleave_c(2, "v")
+            broadcast_virt(1)
+            for i in range(1, 3):
+                quantize_c(i)
+            broadcast_scale()
+            for i in range(2):
+                interleave_f(0, i, "s")
+            for i in range(5):
+                widen_s(i)
+            for i in range(2):
+                turn_s(0, i)
+            quantize_f(0, 0)
+            interleave_f(0, 2, "v")
+            for i in range(2):
+                turned_s_out(0, i, "s")
+            widen_s(5)
+            interleave_f(1, 0, "s")
+            for i in range(1, 3):
+                quantize_f(0, i)
             turn_s(1, 0)
-            group_f(1, 1, "v")
-            group_f(0, 1, "s")
-            quant_f(0, 1)
-            group_f(1, 2, "s")
-            group_f(2, 1, "v")
-            group_f(2, 2, "s")
-            quant_f(1, 1)
-            turn_s(1, 1)
-            half_mm(0, [3], range(G))
-            h_out(0, 3, "s")
-            half_mm(0, [0], range(G))
-            half_mm(0, [2], range(G))
-            quant_f(2, 1)
-            half_mm(0, [1], range(G))
-            group_f(0, 2, "v")
-            half_mm(1, [3], range(G))
-            h_out(0, 0, "s")
-            half_mm(1, [0], range(G))
-            h_out(0, 1, "s")
-            half_mm(1, [1], range(G))
-            h_out(0, 2, "s")
-            quant_f(1, 2)
-            half_mm(1, [2], range(G))
-            quant_f(2, 2)
-            quant_f(0, 2)
-            half_mm(2, [1], range(G))
-            group_h(0, "v")
-            quant_s(0)
-            h_out(1, 3, "s")
-            quant_h(0)
-            product(9)
-            turned_out("s", 1, 1, "s")
-            h_out(1, 0, "s")
-            h_out(1, 1, "s")
-            half_mm(2, [3], range(G))
-            h_out(1, 2, "s")
-            product(8)
-            turned_out("s", 1, 0, "s")
-            product(11)
-            h_out(2, 1, "s")
-            spf_mm(0, 2)
-            product(10)
-            spf_mm(0, 3)
-            spf_out(0, 2, "s")
-            spf_out(0, 3, "s")
-            spf_mm(0, 0)
-            spf_out(0, 0, "s")
-            spf_mm(0, 1)
-            spf_out(0, 1, "s")
-            half_mm(2, [2], range(G))
-            h_out(2, 2, "s")
-            turn_s(2, 0)
-            turn_s(2, 1)
-            turned_out("s", 2, 0, "s")
-            h_out(2, 3, "s")
-            quant_s(1)
-            spf_mm(0, 7)
-            spf_mm(0, 6)
-            group_h(1, "v")
-            spf_out(0, 7, "v")
-            half_mm(2, [0], range(G))
-            turned_out("s", 2, 1, "s")
+            for i in range(6, 8):
+                widen_s(i)
+            for i in range(4):
+                half_mm(0, i)
+            interleave_f(2, 0, "s")
+            interleave_f(1, 1, "v")
+            for i in range(2):
+                quantize_f(1, i)
+            turned_s_out(1, 0, "s")
+            interleave_f(1, 2, "v")
+            for i in range(4):
+                h_out(0, i, "s")
+            widen_s(8)
             turn_h(0, 0)
-            turn_h(2, 1)
-            spf_out(0, 6, "s")
-            quant_h(1)
-            spf_mm(1, 1)
-            square(2)
-            h_out(2, 0, "v")
-            spf_mm(1, 0)
-            spf_mm(1, 5)
-            spf_mm(1, 4)
-            quant_s(2)
-            spf_mm(1, 11)
-            spf_out(1, 1, "s")
-            spf_mm(0, 10)
-            spf_out(1, 0, "s")
-            spf_out(1, 5, "s")
-            spf_out(1, 4, "s")
-            spf_mm(1, 10)
-            spf_out(1, 10, "s")
-            spf_mm(0, 11)
-            spf_out(0, 11, "s")
-            group_h(2, "v")
-            spf_out(1, 11, "v")
-            quant_h(2)
-            spf_out(0, 10, "v")
-            spf_mm(0, 9)
-            spf_out(0, 9, "s")
-            spf_mm(0, 8)
-            spf_mm(1, 3)
-            spf_out(1, 3, "s")
-            spf_out(0, 8, "v")
-            spf_mm(1, 2)
-            spf_out(1, 2, "v")
-            spf_mm(1, 7)
-            spf_mm(2, 6)
-            turned_out("h", 2, 1, "s")
-            spf_out(2, 6, "v")
-            turned_out("h", 0, 0, "s")
-            spf_mm(2, 3)
-            spf_mm(2, 7)
-            spf_mm(2, 2)
-            turn_h(1, 0)
-            spf_out(2, 3, "v")
-            spf_out(2, 7, "s")
-            turn_h(1, 1)
-            spf_out(1, 7, "s")
-            side(0)
-            spf_mm(1, 6)
-            turned_out("h", 1, 1, "s")
-            turned_out("h", 1, 0, "v")
-            spf_out(1, 6, "s")
-            spf_out(2, 2, "v")
+            quantize_f(1, 2)
+            turn_s(1, 1)
+            widen_s(9)
+            gap_root(0)
+            for i in range(3):
+                half_mm(1, i)
+            interleave_h(0, "v")
+            turned_s_out(1, 1, "s")
+            quantize_s(0)
+            gap_square(0)
+            quantize_h(0)
+            widen_s(10)
+            for i in range(2):
+                h_out(1, i, "s")
+            for i in range(4):
+                spf_mm(0, i)
+            quantize_s(1)
+            quantize_f(2, 0)
+            for i in range(4):
+                spf_out(0, i, "s")
+            for i in range(4, 6):
+                spf_mm(0, i)
+            turned_h_out(0, 0, "v")
+            widen_s(11)
+            for i in range(2):
+                turn_s(2, i)
+            for i in range(1, 3):
+                interleave_f(2, i, "v")
+            for i in range(4, 6):
+                spf_out(0, i, "s")
+            half_mm(1, 3)
+            for i in range(2):
+                turned_s_out(2, i, "s")
+            for i in range(6, 8):
+                spf_mm(0, i)
+            for i in range(1, 3):
+                quantize_f(2, i)
             turn_h(0, 1)
-            side(2)
-            root(0)
+            for i in range(2, 4):
+                h_out(1, i, "s")
+            turn_h(1, 0)
+            spf_out(0, 6, "v")
+            half_mm(2, 0)
+            quantize_s(2)
+            spf_out(0, 7, "s")
+            interleave_h(1, "v")
+            gap_root(1)
+            for i in range(8, 12):
+                spf_mm(0, i)
+            for i in range(8, 10):
+                spf_out(0, i, "s")
+            gap_side(0)
+            half_mm(2, 1)
+            quantize_h(1)
+            spf_out(0, 10, "v")
+            spf_out(0, 11, "s")
+            for i in range(4):
+                spf_mm(1, i)
+            h_out(2, 0, "v")
+            turned_h_out(0, 1, "s")
+            spf_out(1, 0, "s")
+            for i in range(1, 3):
+                spf_out(1, i, "v")
+            for i in range(4, 6):
+                spf_mm(1, i)
+            turned_h_out(1, 0, "s")
+            half_mm(2, 2)
+            spf_out(1, 3, "s")
+            spf_out(1, 4, "v")
+            quantize_ht(0)
+            spf_out(1, 5, "s")
+            spf_mm(1, 6)
+            half_mm(2, 3)
+            for i in range(1, 4):
+                h_out(2, i, "v")
+            gap_root(2)
+            for i in range(7, 9):
+                spf_mm(1, i)
+            for i in range(6, 8):
+                spf_out(1, i, "s")
+            turn_h(1, 1)
+            gap_side(1)
+            for i in range(9, 12):
+                spf_mm(1, i)
+            interleave_h(2, "v")
+            gap_square(1)
             turn_h(2, 0)
-            turned_out("h", 2, 0, "s")
-            spf_mm(2, 4)
-            spf_out(2, 4, "s")
-            spf_mm(2, 5)
-            spf_out(2, 5, "s")
-            turned_out("h", 0, 1, "v")
-            spf_mm(1, 8)
-            spf_mm(2, 9)
-            spf_out(2, 9, "s")
-            spf_mm(2, 8)
-            spf_out(2, 8, "s")
-            square(0)
-            quant_ht(1)
-            spf_mm(0, 5)
+            turned_h_out(1, 1, "s")
             spf_out(1, 8, "s")
-            quant_ht(0)
-            spf_mm(1, 9)
-            quant_ht(2)
-            spf_out(1, 9, "s")
-            kappa_mm(2, 1)
-            recip(2)
-            kappa_mm(2, 0)
-            side(1)
-            kappa_out(2, 1)
-            kappa_mm(0, 1)
-            recip(0)
-            root(1)
-            square(1)
-            kappa_out(2, 0)
-            kappa_mm(0, 0)
-            spf_mm(0, 4)
-            kappa_out(0, 1)
-            kappa_out(0, 0)
-            spf_mm(2, 1)
-            spf_out(0, 5, "s")
-            recip(1)
-            spf_out(0, 4, "s")
+            spf_out(1, 9, "v")
+            quantize_h(2)
+            turn_h(2, 1)
+            for i in range(2):
+                turned_h_out(2, i, "s")
+            for i in range(4):
+                spf_mm(2, i)
+            spf_out(1, 10, "s")
+            spf_out(1, 11, "v")
+            for i in range(1, 3):
+                quantize_ht(i)
+            for i in range(4, 6):
+                spf_mm(2, i)
+            for i in range(5):
+                spf_out(2, i, "s")
+            for i in range(2):
+                gap_sign(i)
+            for i in range(2):
+                kappa_mm(0, i)
+            for i in range(2):
+                kappa_out(0, i)
+            for i in range(6, 8):
+                spf_mm(2, i)
+            for i in range(5, 7):
+                spf_out(2, i, "s")
             kappa_mm(1, 0)
-            root(3)
-            square(3)
-            kappa_mm(1, 1)
-            spf_mm(2, 0)
-            side(3)
-            spf_out(2, 1, "s")
+            spf_out(2, 7, "v")
+            gap_square(2)
+            for i in range(8, 10):
+                spf_mm(2, i)
+            gap_side(2)
             kappa_out(1, 0)
-            spf_mm(2, 11)
-            spf_out(2, 0, "s")
-            spf_mm(2, 10)
-            kappa_mm(3, 1)
+            kappa_mm(1, 1)
+            for i in range(2):
+                kappa_mm(2, i)
+            for i in range(8, 10):
+                spf_out(2, i, "s")
+            gap_sign(2)
+            gap_root(3)
             kappa_out(1, 1)
-            kappa_mm(3, 0)
-            recip(3)
-            kappa_out(3, 1)
-            spf_out(2, 11, "s")
-            spf_out(2, 10, "s")
-            kappa_out(3, 0)
+            gap_side(3)
+            gap_square(3)
+            for i in range(2):
+                kappa_out(2, i)
+            for i in range(10, 12):
+                spf_mm(2, i)
+            for i in range(2):
+                kappa_mm(3, i)
+            for i in range(10, 12):
+                spf_out(2, i, "s")
+            gap_sign(3)
+            for i in range(2):
+                kappa_out(3, i)

from contextlib import ExitStack

import concourse.mybir as mybir
from concourse.masks import make_identity

F32 = mybir.dt.float32
BF16 = mybir.dt.bfloat16
I32 = mybir.dt.int32
U32 = mybir.dt.uint32
U8 = mybir.dt.uint8
FP8 = mybir.dt.float8_e4m3fn
FP8X4 = mybir.dt.float8_e4m3fn_x4
FP4X4 = mybir.dt.float4_e2m1fn_x4
ACT = mybir.ActivationFunctionType
ALU = mybir.AluOpType

P = 128
PACK = 4
B, O, V = 1536, 512, 1024
COLS = 512
G = B // (P * PACK)
ROWS = B // P
HALF_ROWS = ROWS // 2

FLOPS = 2 * O * B * B + 2 * O * B * V + 2 * B * O * B


def tile_orbital_rotation_gradient_s8_kernel(
    tc, c_occ, fock, occ, c_virt_words, c_virt_scales, sc_bytes, sc_scale, e_occ, e_virt, kappa, spf
):
    nc = tc.nc
    with ExitStack() as ctx:
        keep = ctx.enter_context(tc.tile_pool(name="keep", bufs=1))
        work = ctx.enter_context(tc.tile_pool(name="work", bufs=3))
        big = ctx.enter_context(tc.tile_pool(name="big", bufs=12))
        mm = ctx.enter_context(tc.psum_pool(name="mm", bufs=6))
        tr = ctx.enter_context(tc.psum_pool(name="tr", bufs=2))

        scale_row = keep.tile([P, O], F32, name="scale_row")
        virt_row = keep.tile([P, V], BF16, name="virt_row")
        ones_f = keep.tile([P, P], F32, name="ones_f")
        ones_b = keep.tile([P, P], BF16, name="ones_b")
        ident = keep.tile([P, P], F32, name="ident")
        scale_all = keep.tile([P, O], F32, name="scale_all")
        virt_all = keep.tile([P, V], BF16, name="virt_all")
        per_orbital_b = keep.tile([P, 2, 16], BF16, name="per_orbital_b")
        per_orbital = keep.tile([P, 2, PACK], F32, name="per_orbital")
        first_function = keep.tile([P, 1], F32, name="first_function")

        c_raw = [big.tile([P, PACK, O], BF16, name="big4k") for g in range(G)]
        f_raw_first = [big.tile([P, PACK, COLS], BF16, name="big4k") for g in range(G)]
        f_raw_rest = [keep.tile([P, PACK, B - COLS], BF16, name=f"f_raw_rest{g}") for g in range(G)]
        s_raw = [keep.tile([P, HALF_ROWS, O], U8, name=f"s_raw{k}") for k in range(2)]
        cv_words = keep.tile([P, G, 2 * V], U8, name="cv_words", align_bytes=64)
        cv_scales = keep.tile([P, G, V], U8, name="cv_scales", align_bytes=64)

        c_codes = keep.tile([P, G, O], U32, name="c_codes", align_bytes=64)
        c_scales = keep.tile([P, G, O], U8, name="c_scales", align_bytes=64)
        f_codes = keep.tile([P, G, B], U32, name="f_codes", align_bytes=64)
        f_scales = keep.tile([P, G, B], U8, name="f_scales", align_bytes=64)
        h_codes = keep.tile([P, B], U32, name="h_codes", align_bytes=64)
        h_scales = keep.tile([P, B], U8, name="h_scales", align_bytes=64)
        ht_codes = keep.tile([P, G, O], U32, name="ht_codes", align_bytes=64)
        ht_scales = keep.tile([P, G, O], U8, name="ht_scales", align_bytes=64)
        s_codes = keep.tile([P, B], U32, name="s_codes", align_bytes=64)
        s_scales = keep.tile([P, B], U8, name="s_scales", align_bytes=64)

        h_bf = keep.tile([P, PACK, B], BF16, name="h_bf", align_bytes=64)
        below = keep.tile([P, PACK, V], BF16, name="below")
        rgap = keep.tile([P, PACK, V], F32, name="rgap")

        c_view = c_occ.rearrange("(g p j) o -> g p j o", p=P, j=PACK)
        f_view = fock.rearrange("(g p j) n -> g p j n", p=P, j=PACK)
        s_view = sc_bytes.rearrange("(p i) o -> p i o", i=ROWS)
        spf_view = spf.rearrange("(p i) n -> p i n", i=ROWS)
        kappa_view = kappa.rearrange("(p t) v -> p t v", t=PACK)

        def block(n):
            return slice(n * COLS, (n + 1) * COLS)

        def copy(engine, out, in_):
            if engine == "v":
                nc.vector.tensor_copy(out=out, in_=in_)
            else:
                nc.scalar.copy(out=out, in_=in_)

        def quantize(source, codes, scales):
            nc.vector.quantize_mx(
                out=codes.bitcast(FP8X4), scales=scales, in_=source[:].rearrange("p c j -> p (c j)")
            )

        def broadcast_scale():
            ps = mm.tile([P, COLS], F32, name="ps")
            nc.tensor.matmul(out=ps[:], lhsT=ones_f[:], rhs=scale_row[:], start=True, stop=True)
            nc.scalar.copy(out=scale_all[:], in_=ps[:])

        def broadcast_virt(v):
            ps = mm.tile([P, COLS], F32, name="ps")
            nc.tensor.matmul(out=ps[:], lhsT=ones_b[:], rhs=virt_row[:, block(v)], start=True, stop=True)
            nc.scalar.copy(out=virt_all[:, block(v)], in_=ps[:])

        interleaved = {}

        def new_interleaved(key):
            tile = work.tile([P, COLS, PACK], BF16, name="interleaved", align_bytes=64, bufs=5)
            interleaved[key] = tile
            return tile

        def interleave_by_four(tile, source, engine):
            copy(
                engine,
                tile[:].rearrange("p (c i) j -> p c j i", i=4),
                source.rearrange("p j (c i) -> p c j i", i=4),
            )

        def interleave_c(g, engine):
            copy(
                engine,
                new_interleaved(("c", g))[:].rearrange("p (t m) j -> p t m j", t=PACK),
                c_raw[g][:].rearrange("p j (m t) -> p t m j", t=PACK),
            )

        def quantize_c(g):
            quantize(interleaved["c", g], c_codes[:, g, :], c_scales[:, g, :])

        def interleave_f(n, g, engine):
            source = f_raw_first[g][:] if n == 0 else f_raw_rest[g][:, :, block(n - 1)]
            interleave_by_four(new_interleaved(("f", n, g)), source, engine)

        def quantize_f(n, g):
            quantize(interleaved["f", n, g], f_codes[:, g, block(n)], f_scales[:, g, block(n)])

        def interleave_h(n, engine):
            interleave_by_four(new_interleaved(("h", n)), h_bf[:, :, block(n)], engine)

        def quantize_h(n):
            quantize(interleaved["h", n], h_codes[:, block(n)], h_scales[:, block(n)])

        half = {}

        def half_mm(n, t):
            ps = mm.tile([P, COLS], F32, name="ps")
            half[n, t] = ps
            orbitals = slice(t * P, (t + 1) * P)
            for g in range(G):
                nc.tensor.matmul_mx(
                    out=ps[:],
                    lhsT=c_codes[:, g, orbitals].bitcast(FP8X4),
                    lhsT_scale=c_scales[:, g, orbitals],
                    rhs=f_codes[:, g, block(n)].bitcast(FP8X4),
                    rhs_scale=f_scales[:, g, block(n)],
                    start=(g == 0),
                    stop=(g == G - 1),
                )

        def h_out(n, t, engine):
            out, factor = h_bf[:, t, block(n)], per_orbital[:, 0, t : t + 1]
            if engine == "v":
                nc.vector.tensor_scalar(out=out, in0=half[n, t][:], scalar1=factor, scalar2=None, op0=ALU.mult)
            else:
                nc.scalar.activation(out=out, in_=half[n, t][:], func=ACT.Copy, scale=factor)

        in_psum, turned = {}, {}

        def turn(key, rows):
            ps = tr.tile([P, 4, P], F32, name="pt")
            in_psum[key] = ps
            for k in range(2):
                words = rows[k].bitcast(F32)
                for u in range(2):
                    nc.tensor.transpose(ps[:, 2 * k + u, :], words[:, u : COLS // 2 : 2], ident[:])

        def turned_out(key, engine):
            what, pair = key[:2], key[2]
            if what not in turned:
                tile = work.tile([P, COLS, PACK], BF16, name="turned", align_bytes=64, bufs=4)
                turned[what] = tile
            words = turned[what][:].rearrange("p c j -> p (c j)").bitcast(F32)
            copy(
                engine,
                words[:, block(pair)].rearrange("p (k r u) -> p k r u", k=2, u=2),
                in_psum[key][:].rearrange("p (k u) r -> p k r u", k=2),
            )

        def turn_h(n, pair):
            turn(("h", n, pair), [h_bf[:, 2 * pair + k, block(n)] for k in range(2)])

        def turned_h_out(n, pair, engine):
            turned_out(("h", n, pair), engine)

        def quantize_ht(n):
            quantize(turned["h", n], ht_codes[:, n, :], ht_scales[:, n, :])

        s_bf = {}

        def widen_s(i):
            if i // 4 not in s_bf:
                tile = work.tile([P, 4, O], BF16, name="s_bf")
                s_bf[i // 4] = tile
            nc.vector.tensor_tensor(
                out=s_bf[i // 4][:, i % 4, :],
                in0=s_raw[i // HALF_ROWS][:, i % HALF_ROWS, :].bitcast(FP8),
                in1=scale_all[:],
                op=ALU.mult,
            )

        def turn_s(chunk, pair):
            turn(("s", chunk, pair), [s_bf[chunk][:, 2 * pair + k, :] for k in range(2)])

        def turned_s_out(chunk, pair, engine):
            turned_out(("s", chunk, pair), engine)

        def quantize_s(chunk):
            quantize(turned["s", chunk], s_codes[:, block(chunk)], s_scales[:, block(chunk)])

        product, result = {}, {}

        def spf_mm(n, i):
            ps = mm.tile([P, COLS], F32, name="ps")
            product[n, i] = ps
            rows = slice(i * P, (i + 1) * P)
            nc.tensor.matmul_mx(
                out=ps[:],
                lhsT=s_codes[:, rows].bitcast(FP8X4),
                lhsT_scale=s_scales[:, rows],
                rhs=h_codes[:, block(n)].bitcast(FP8X4),
                rhs_scale=h_scales[:, block(n)],
                start=True,
                stop=True,
            )

        def spf_out(n, i, engine):
            pair = (n, i // 2)
            if pair not in result:
                tile = big.tile([P, 2, COLS], F32, name="big4k")
                result[pair] = tile
            copy(engine, result[pair][:, i % 2, :], product[n, i][:])
            if i % 2:
                nc.sync.dma_start(out=spf_view[:, i - 1 : i + 1, block(n)], in_=result[pair][:])

        def gap_root(t):
            nc.scalar.activation(
                out=rgap[:, t, :],
                in_=virt_all[:],
                func=ACT.Abs_reciprocal_sqrt,
                scale=-1.0,
                bias=per_orbital[:, 1, t : t + 1],
            )

        def gap_square(t):
            nc.scalar.activation(out=rgap[:, t, :], in_=rgap[:, t, :], func=ACT.Square)

        def gap_side(t):
            nc.vector.tensor_scalar(
                out=below[:, t, :],
                in0=virt_all[:],
                scalar1=per_orbital[:, 1, t : t + 1],
                scalar2=2.0,
                op0=ALU.is_lt,
                op1=ALU.mult,
            )

        def gap_sign(t):
            nc.vector.scalar_tensor_tensor(
                out=rgap[:, t, :], in0=below[:, t, :], scalar=1.0, in1=rgap[:, t, :], op0=ALU.subtract, op1=ALU.mult
            )

        grad = {}

        def kappa_mm(t, v):
            ps = mm.tile([P, COLS], F32, name="ps")
            grad[t, v] = ps
            orbitals = slice(t * P, (t + 1) * P)
            for g in range(G):
                nc.tensor.matmul_mx(
                    out=ps[:],
                    lhsT=ht_codes[:, g, orbitals].bitcast(FP8X4),
                    lhsT_scale=ht_scales[:, g, orbitals],
                    rhs=cv_words[:, g, 2 * COLS * v : 2 * COLS * (v + 1)].bitcast(FP4X4),
                    rhs_scale=cv_scales[:, g, block(v)],
                    start=(g == 0),
                    stop=(g == G - 1),
                )

        def kappa_out(t, v):
            nc.vector.tensor_tensor(
                out=rgap[:, t, block(v)], in0=grad[t, v][:], in1=rgap[:, t, block(v)], op=ALU.mult
            )
            if t == PACK - 1:
                nc.sync.dma_start(out=kappa_view[:, t, block(v)], in_=rgap[:, t, block(v)])
            elif v == 1:
                nc.sync.dma_start(out=kappa_view[:, t, :], in_=rgap[:, t, :])

        with tc.manual_schedule():
            nc.vector.memset(scale_row[:], 0.0)
            nc.vector.memset(ones_f[:], 1.0)
            nc.vector.memset(virt_row[:], 0.0)
            nc.vector.memset(ones_b[:], 1.0)
            nc.vector.memset(first_function[:], 1.0)
            nc.vector.memset(cv_scales[:].rearrange("p g v -> p (g v)").bitcast(I32), 0)
            make_identity(nc, ident[:])
            nc.scalar.activation(out=first_function[:], in_=first_function[:], func=ACT.Abs_reciprocal_sqrt)

            nc.sync.dma_start(out=c_raw[0][:], in_=c_view[0])
            nc.sync.dma_start(out=scale_row[0:1, :], in_=sc_scale)
            nc.sync.dma_start(out=virt_row[0:1, :], in_=e_virt.rearrange("(o v) -> o v", o=1))
            nc.sync.dma_start(out=per_orbital_b[:, 1, :PACK], in_=e_occ.rearrange("(p t) -> p t", t=PACK))
            nc.sync.dma_start(out=per_orbital_b[:, 0, :PACK], in_=occ.rearrange("(p t) -> p t", t=PACK))
            for g in range(1, G):
                nc.sync.dma_start(out=c_raw[g][:], in_=c_view[g])
            nc.sync.dma_start(out=s_raw[0][:], in_=s_view[:, :HALF_ROWS, :])
            for g in range(G):
                nc.sync.dma_start(out=f_raw_first[g][:], in_=f_view[g, :, :, :COLS])
            nc.sync.dma_start(out=s_raw[1][:], in_=s_view[:, HALF_ROWS:, :])
            for g in range(G):
                nc.sync.dma_start(out=f_raw_rest[g][:], in_=f_view[g, :, :, COLS:])
            nc.sync.dma_start(out=cv_words[:], in_=c_virt_words.rearrange("g p n -> p g n"))
            for q in range(4):
                nc.sync.dma_start(
                    out=cv_scales[32 * q : 32 * q + 4, :, :].bitcast(I32),
                    in_=c_virt_scales[:, 4 * q : 4 * q + 4, :].bitcast(I32).rearrange("g q v -> q g v"),
                )

            interleave_c(0, "v")
            nc.vector.tensor_copy(out=per_orbital[:], in_=per_orbital_b[:, :, :PACK])
            broadcast_virt(0)
            interleave_c(1, "s")
            quantize_c(0)
            interleave_c(2, "v")
            broadcast_virt(1)
            for i in range(1, 3):
                quantize_c(i)
            broadcast_scale()
            for i in range(2):
                interleave_f(0, i, "s")
            for i in range(5):
                widen_s(i)
            for i in range(2):
                turn_s(0, i)
            quantize_f(0, 0)
            interleave_f(0, 2, "v")
            for i in range(2):
                turned_s_out(0, i, "s")
            widen_s(5)
            interleave_f(1, 0, "s")
            for i in range(1, 3):
                quantize_f(0, i)
            turn_s(1, 0)
            for i in range(6, 8):
                widen_s(i)
            for i in range(4):
                half_mm(0, i)
            interleave_f(2, 0, "s")
            interleave_f(1, 1, "v")
            for i in range(2):
                quantize_f(1, i)
            turned_s_out(1, 0, "s")
            interleave_f(1, 2, "v")
            for i in range(4):
                h_out(0, i, "s")
            widen_s(8)
            turn_h(0, 0)
            quantize_f(1, 2)
            turn_s(1, 1)
            widen_s(9)
            gap_root(0)
            for i in range(3):
                half_mm(1, i)
            interleave_h(0, "v")
            turned_s_out(1, 1, "s")
            quantize_s(0)
            gap_square(0)
            quantize_h(0)
            widen_s(10)
            for i in range(2):
                h_out(1, i, "s")
            for i in range(4):
                spf_mm(0, i)
            quantize_s(1)
            quantize_f(2, 0)
            for i in range(4):
                spf_out(0, i, "s")
            for i in range(4, 6):
                spf_mm(0, i)
            turned_h_out(0, 0, "v")
            widen_s(11)
            for i in range(2):
                turn_s(2, i)
            for i in range(1, 3):
                interleave_f(2, i, "v")
            for i in range(4, 6):
                spf_out(0, i, "s")
            half_mm(1, 3)
            for i in range(2):
                turned_s_out(2, i, "s")
            for i in range(6, 8):
                spf_mm(0, i)
            for i in range(1, 3):
                quantize_f(2, i)
            turn_h(0, 1)
            for i in range(2, 4):
                h_out(1, i, "s")
            turn_h(1, 0)
            spf_out(0, 6, "v")
            half_mm(2, 0)
            quantize_s(2)
            spf_out(0, 7, "s")
            interleave_h(1, "v")
            gap_root(1)
            for i in range(8, 12):
                spf_mm(0, i)
            for i in range(8, 10):
                spf_out(0, i, "s")
            gap_side(0)
            half_mm(2, 1)
            quantize_h(1)
            spf_out(0, 10, "v")
            spf_out(0, 11, "s")
            for i in range(4):
                spf_mm(1, i)
            h_out(2, 0, "v")
            turned_h_out(0, 1, "s")
            spf_out(1, 0, "s")
            for i in range(1, 3):
                spf_out(1, i, "v")
            for i in range(4, 6):
                spf_mm(1, i)
            turned_h_out(1, 0, "s")
            half_mm(2, 2)
            spf_out(1, 3, "s")
            spf_out(1, 4, "v")
            quantize_ht(0)
            spf_out(1, 5, "s")
            spf_mm(1, 6)
            half_mm(2, 3)
            for i in range(1, 4):
                h_out(2, i, "v")
            gap_root(2)
            for i in range(7, 9):
                spf_mm(1, i)
            for i in range(6, 8):
                spf_out(1, i, "s")
            turn_h(1, 1)
            gap_side(1)
            for i in range(9, 12):
                spf_mm(1, i)
            interleave_h(2, "v")
            gap_square(1)
            turn_h(2, 0)
            turned_h_out(1, 1, "s")
            spf_out(1, 8, "s")
            spf_out(1, 9, "v")
            quantize_h(2)
            turn_h(2, 1)
            for i in range(2):
                turned_h_out(2, i, "s")
            for i in range(4):
                spf_mm(2, i)
            spf_out(1, 10, "s")
            spf_out(1, 11, "v")
            for i in range(1, 3):
                quantize_ht(i)
            for i in range(4, 6):
                spf_mm(2, i)
            for i in range(5):
                spf_out(2, i, "s")
            for i in range(2):
                gap_sign(i)
            for i in range(2):
                kappa_mm(0, i)
            for i in range(2):
                kappa_out(0, i)
            for i in range(6, 8):
                spf_mm(2, i)
            for i in range(5, 7):
                spf_out(2, i, "s")
            kappa_mm(1, 0)
            spf_out(2, 7, "v")
            gap_square(2)
            for i in range(8, 10):
                spf_mm(2, i)
            gap_side(2)
            kappa_out(1, 0)
            kappa_mm(1, 1)
            for i in range(2):
                kappa_mm(2, i)
            for i in range(8, 10):
                spf_out(2, i, "s")
            gap_sign(2)
            gap_root(3)
            kappa_out(1, 1)
            gap_side(3)
            gap_square(3)
            for i in range(2):
                kappa_out(2, i)
            for i in range(10, 12):
                spf_mm(2, i)
            for i in range(2):
                kappa_mm(3, i)
            for i in range(10, 12):
                spf_out(2, i, "s")
            gap_sign(3)
            for i in range(2):
                kappa_out(3, i)
